import numpy as np
import ml_dtypes


def mxq(x, axis, fmt="e4m3"):
    dtype, down = {"e4m3": (ml_dtypes.float8_e4m3fn, 7), "e5m2": (ml_dtypes.float8_e5m2, 14)}[fmt]
    v = np.moveaxis(np.asarray(x, np.float32).astype(ml_dtypes.bfloat16).astype(np.float64), axis, -1)
    blocks = v.reshape(v.shape[:-1] + (-1, 32))
    amax = np.abs(blocks).max(-1, keepdims=True)
    byte = np.maximum(np.where(amax > 0, np.frexp(amax)[1] - 1 + 127, 0) - down, 1)
    scale = np.exp2(byte - 127.0)
    codes = (blocks / scale).astype(np.float32).astype(dtype).astype(np.float64)
    return np.moveaxis((codes * scale).reshape(v.shape), -1, axis)


WIDE = False


def mx_kscale(k, group=512):
    if not WIDE:
        return np.ones(k)
    levels = np.array([10, -10, 5, -5, 0])
    if group != 512:
        return np.exp2(np.random.permutation(np.resize(levels, k // group))).repeat(group)
    if k % 512:
        return np.exp2(np.random.permutation(np.resize(levels, k // 32))).repeat(32)
    a = np.empty((k // 512, 16))
    for p in range(k // 512):
        a[p, :8] = np.random.permutation(np.resize(levels, 8))
        for g in range(8):
            far = levels[np.abs(levels - a[p, g]) >= 10]
            a[p, g + 8] = far[np.random.randint(len(far))]
    return np.exp2(a.ravel()).repeat(32)


def f64(x):
    return np.asarray(x).astype(np.float64)


def striped(idx):
    return np.tile(np.asarray(idx).reshape(-1, 16).T, (8, 1)).astype(np.uint16)


def unstriped(offs):
    return offs[:16].T.reshape(-1).astype(np.int64)


H, KV, D, NQ, N = 8, 2, 128, 512, 512
CAP = 2.0


def setup_inputs():
    n = np.random.standard_normal
    s = mx_kscale(D, 0)[:, None]
    u = mx_kscale(N)
    t = np.random.uniform(0.5, 2.0, N) * u
    v = n((KV, N, 128))
    v[:, :, 127] = 1.0
    return {
        "qT": (n((H, D, NQ)) * s * (0.70 / np.sqrt(D))).astype(np.float32),
        "kT": (n((KV, D, N)) / s).astype(np.float32),
        "t": t.reshape(N, 1).astype(np.float32),
        "v": (v / t[:, None]).astype(np.float32),
        "sink": (N * np.random.uniform(0.1, 1.0, (H, NQ, 1))).astype(np.float32),
        "og": n((H, NQ, 128)).astype(np.float32),
    }


def reference(qT, kT, t, v, sink, og):
    a = np.repeat(mxq(f64(kT), 1, "e4m3"), H // KV, 0).transpose(0, 2, 1) @ mxq(f64(qT), 1, "e4m3")
    a = CAP * np.tanh(a / CAP)
    p = np.exp(a)
    w = p * f64(t)
    y = mxq(w, 1, "e4m3").transpose(0, 2, 1) @ np.repeat(mxq(f64(v), 1, "e4m3"), H // KV, 0)
    y = y / (y[:, :, 127:128] + f64(sink))
    y = y / (1.0 + np.exp(-f64(og)))
    return y

@@ -1,0 +1,354 @@
+from contextlib import ExitStack
+
+import concourse.mybir as mybir
+
+H, KV, D, NQ, NT = 8, 2, 128, 512, 512
+CAP = 2.0
+FLOPS = 2 * 2 * H * NQ * NT * D
+
+F32 = mybir.dt.float32
+BF16 = mybir.dt.bfloat16
+U32 = mybir.dt.uint32
+U8 = mybir.dt.uint8
+FP8X4 = mybir.dt.float8_e4m3fn_x4
+ACT = mybir.ActivationFunctionType
+ALU = mybir.AluOpType
+
+P = 128
+PACK = 4
+ROWS = 32
+G = 4
+QT = 128
+CH = NQ // QT
+UNITS = KV * CH
+BIG = 2.0**62
+DEPTH = 3
+
+
+def tile_rows_a_exp_cap_sink_gate_kernel(tc, qT, kT, t, v, sink, og, out):
+    nc = tc.nc
+    with ExitStack() as ctx:
+        sb = ctx.enter_context(tc.tile_pool(name="sb", bufs=1))
+        ps = ctx.enter_context(tc.psum_pool(name="ps", bufs=1))
+
+        def mk(name, shape, dtype):
+            return sb.tile(shape, dtype, name=name, align_bytes=64)
+
+        t_raw = mk("t_raw", [P, PACK], F32)
+        t_abs = mk("t_abs", [P, PACK], F32)
+        t_fac = mk("t_fac", [P, 3, PACK], F32)
+        t_log = mk("t_log", [P, 3, PACK], F32)
+        t_sum = mk("t_sum", [P, PACK], F32)
+        ln_t = mk("ln_t", [P, PACK], F32)
+        t_pos = mk("t_pos", [P, PACK], F32)
+        t_sgn = mk("t_sgn", [P, PACK], F32)
+        ones = mk("ones", [P, 1], F32)
+        warm = mk("warm", [P, 2], F32)
+        sink_raw = mk("sink_raw", [P, 32], F32)
+        sink_q = mk("sink_q", [P, 32], F32)
+
+        k_raw = [mk("k_raw%d" % s, [P, PACK, NT], F32) for s in range(KV)]
+        k_bf = [mk("k_bf%d" % s, [P, PACK, P, PACK], BF16) for s in range(KV)]
+        k_codes = [mk("k_codes%d" % s, [P, NT], U32) for s in range(KV)]
+        k_scales = [mk("k_scales%d" % s, [P, NT], U8) for s in range(KV)]
+        q_raw = [mk("q_raw%d" % s, [P, PACK, NQ], F32) for s in range(KV)]
+        q_bf = [mk("q_bf%d" % u, [P, QT, PACK], BF16) for u in range(UNITS)]
+        q_codes = [mk("q_codes%d" % u, [P, QT], U32) for u in range(UNITS)]
+        q_scales = [mk("q_scales%d" % u, [P, QT], U8) for u in range(UNITS)]
+        v_raw = [mk("v_raw%d" % s, [P, PACK, D], F32) for s in range(KV)]
+        v_bf = [mk("v_bf%d" % s, [P, D, PACK], BF16) for s in range(KV)]
+        v_codes = [mk("v_codes%d" % s, [P, D], U32) for s in range(KV)]
+        v_scales = [mk("v_scales%d" % s, [P, D], U8) for s in range(KV)]
+        og_raw = [mk("og_raw%d" % s, [P, CH, G, D], F32) for s in range(KV)]
+        g_tanh = [mk("g_tanh%d" % u, [P, G, D], F32) for u in range(UNITS)]
+        gate = [mk("gate%d" % u, [P, G, D], F32) for u in range(UNITS)]
+        res = [mk("res%d" % u, [P, G, D], F32) for u in range(UNITS)]
+        den = [mk("den%d" % u, [P, G], F32) for u in range(UNITS)]
+        rec = [mk("rec%d" % u, [P, G], F32) for u in range(UNITS)]
+        capped = [mk("capped%d" % i, [P, G, PACK, QT], F32) for i in range(2)]
+        w_rows = [mk("w_rows%d" % i, [P, PACK, G * QT], BF16) for i in range(DEPTH)]
+        w_bf = [mk("w_bf%d" % i, [P, G * QT, PACK], BF16) for i in range(2)]
+        w_codes = [mk("w_codes%d" % i, [P, G * QT], U32) for i in range(2)]
+        w_scales = [mk("w_scales%d" % i, [P, G * QT], U8) for i in range(2)]
+
+        score = [ps.tile([P, PACK, QT], F32, name="score%d" % g) for g in range(G)]
+        ybank = [ps.tile([P, G, D], F32, name="ybank%d" % i) for i in range(4)]
+
+        q_view = qT.rearrange("(s g) (p j) n -> s (g p) j n", g=G, j=PACK)
+        k_view = kT.rearrange("s (p j) n -> s p j n", j=PACK)
+        v_view = v.rearrange("s (p j) e -> s p j e", j=PACK)
+        og_view = og.rearrange("(s g) (c p) e -> s c p g e", g=G, p=P)
+        out_view = out.rearrange("(s g) (c p) e -> s c p g e", g=G, p=P)
+
+        def load_q(s, c0, c1):
+            nc.sync.dma_start(out=q_raw[s][:, :, c0 * QT : c1 * QT], in_=q_view[s][:, :, c0 * QT : c1 * QT])
+
+        def load_k(eng, s, g):
+            eng.dma_start(out=k_raw[s][ROWS * g : ROWS * (g + 1)], in_=k_view[s])
+
+        def load_og(u):
+            nc.sync.dma_start(out=og_raw[u // CH][:, u % CH], in_=og_view[u // CH][u % CH])
+
+        def load_v(s):
+            nc.sync.dma_start(out=v_raw[s][:], in_=v_view[s])
+
+        def quant(codes, scales, src):
+            nc.vector.quantize_mx(out=codes.bitcast(FP8X4), scales=scales, in_=src)
+
+        def copy_q(u):
+            src = q_raw[u // CH][:, :, (u % CH) * QT : (u % CH + 1) * QT]
+            nc.vector.tensor_copy(out=q_bf[u][:], in_=src.rearrange("p j n -> p n j"))
+
+        def quant_q(u):
+            quant(q_codes[u][:], q_scales[u][:], q_bf[u][:].rearrange("p n j -> p (n j)"))
+
+        def copy_k(s, half):
+            src = k_raw[s][:].rearrange("p j (m r) -> p r m j", r=PACK)
+            nc.vector.tensor_copy(out=k_bf[s][:, 2 * half : 2 * half + 2], in_=src[:, 2 * half : 2 * half + 2])
+
+        def quant_k(s, half):
+            cols = slice(2 * half * P, (2 * half + 2) * P)
+            src = k_bf[s][:, 2 * half : 2 * half + 2].rearrange("p r m j -> p (r m j)")
+            quant(k_codes[s][:, cols], k_scales[s][:, cols], src)
+
+        def copy_v(s):
+            nc.vector.tensor_tensor(
+                out=v_bf[s][:],
+                in0=v_raw[s][:].rearrange("p r e -> p e r"),
+                in1=t_sgn[:].unsqueeze(1).to_broadcast([P, D, PACK]),
+                op=ALU.mult,
+            )
+
+        def quant_v(s):
+            quant(v_codes[s][:], v_scales[s][:], v_bf[s][:].rearrange("p e r -> p (e r)"))
+
+        def scores(u, g):
+            s = u // CH
+            rows = slice(ROWS * g, ROWS * (g + 1))
+            for r in range(PACK):
+                cols = slice(r * P, (r + 1) * P)
+                nc.tensor.matmul_mx(
+                    out=score[g][:, r, :],
+                    lhsT=k_codes[s][rows, cols].bitcast(FP8X4),
+                    lhsT_scale=k_scales[s][rows, cols],
+                    rhs=q_codes[u][rows, :].bitcast(FP8X4),
+                    rhs_scale=q_scales[u][rows, :],
+                    start=True,
+                    stop=True,
+                )
+
+        def cap(u, g):
+            nc.scalar.activation(
+                out=capped[u % 2][:, g].rearrange("p r n -> p (r n)"),
+                in_=score[g][:].rearrange("p r n -> p (r n)"),
+                func=ACT.Tanh,
+                scale=1.0 / CAP,
+            )
+
+        def weights(u, g0, g1):
+            for r in range(PACK):
+                nc.scalar.activation(
+                    out=w_rows[u % DEPTH][:, r, g0 * QT : g1 * QT].rearrange("p (g n) -> p g n", n=QT),
+                    in_=capped[u % 2][:, g0:g1, r, :],
+                    func=ACT.Exp,
+                    scale=CAP,
+                    bias=ln_t[:, r : r + 1],
+                )
+
+        def gate_tanh(u):
+            nc.scalar.activation(out=g_tanh[u][:], in_=og_raw[u // CH][:, u % CH], func=ACT.Tanh, scale=0.5)
+
+        def gate_affine(u):
+            nc.vector.tensor_scalar(
+                out=gate[u][:], in0=g_tanh[u][:], scalar1=0.5, scalar2=0.5, op0=ALU.mult, op1=ALU.add
+            )
+
+        def copy_w(u, g0, g1):
+            cols = slice(g0 * QT, g1 * QT)
+            nc.vector.tensor_copy(
+                out=w_bf[u % 2][:, cols, :], in_=w_rows[u % DEPTH][:, :, cols].rearrange("p r n -> p n r")
+            )
+
+        def quant_w(u, g0, g1):
+            cols = slice(g0 * QT, g1 * QT)
+            src = w_bf[u % 2][:, cols, :].rearrange("p n r -> p (n r)")
+            quant(w_codes[u % 2][:, cols], w_scales[u % 2][:, cols], src)
+
+        def bank(u, g0):
+            return ybank[0 if (u, g0) == (UNITS - 1, G - 1) else u % 4]
+
+        def values(u, g0, g1):
+            s = u // CH
+            for g in range(g0, g1):
+                cols = slice(g * QT, (g + 1) * QT)
+                nc.tensor.matmul_mx(
+                    out=bank(u, g0)[:, g, :],
+                    lhsT=w_codes[u % 2][:, cols].bitcast(FP8X4),
+                    lhsT_scale=w_scales[u % 2][:, cols],
+                    rhs=v_codes[s][:].bitcast(FP8X4),
+                    rhs_scale=v_scales[s][:],
+                    start=True,
+                    stop=True,
+                )
+
+        def denom(u, g0, g1):
+            s, c = divmod(u, CH)
+            sk = sink_q[:].rearrange("p (s g c) -> p s c g", s=KV, g=G)
+            nc.vector.tensor_tensor(
+                out=den[u][:, g0:g1], in0=bank(u, g0)[:, g0:g1, D - 1], in1=sk[:, s, c, g0:g1], op=ALU.add
+            )
+
+        def recip(u, g0, g1):
+            nc.vector.reciprocal(out=rec[u][:, g0:g1], in_=den[u][:, g0:g1])
+
+        def finish(u, g0, g):
+            nc.vector.scalar_tensor_tensor(
+                out=res[u][:, g, :],
+                in0=bank(u, g0)[:, g, :],
+                scalar=rec[u][:, g : g + 1],
+                in1=gate[u][:, g, :],
+                op0=ALU.mult,
+                op1=ALU.mult,
+            )
+
+        def store(u, g0, g1):
+            nc.sync.dma_start(out=out_view[u // CH][u % CH][:, g0:g1, :], in_=res[u][:, g0:g1, :])
+
+        ctx.enter_context(tc.manual_schedule())
+
+        nc.scalar.dma_start(out=t_raw[:], in_=t.rearrange("(p r) o -> p (r o)", r=PACK))
+        load_q(0, 0, 1)
+        load_k(nc.scalar, 0, 2)
+        load_k(nc.sync, 0, 0)
+        load_k(nc.scalar, 0, 3)
+        load_k(nc.sync, 0, 1)
+        for u in range(3):
+            load_og(u)
+        load_q(0, 1, 2)
+        load_v(0)
+        load_og(3)
+        load_q(0, 2, 4)
+        nc.sync.dma_start(out=sink_raw[:], in_=sink.rearrange("h (c a j) o -> a (h c) (j o)", c=CH, a=4))
+        for g in (0, 2, 1, 3):
+            load_k(nc.sync, 1, g)
+        load_og(4)
+        load_q(1, 0, 4)
+        load_og(5)
+        load_og(6)
+        load_v(1)
+        load_og(7)
+
+        nc.gpsimd.memset(ones[:], 1.0)
+        nc.scalar.activation(out=warm[:, 0:1], in_=ones[:], func=ACT.Ln)
+        nc.vector.scalar_tensor_tensor(out=t_abs[:], in0=t_raw[:], scalar=-1.0, in1=t_raw[:], op0=ALU.mult, op1=ALU.max)
+        nc.vector.tensor_scalar(out=t_pos[:], in0=t_raw[:], scalar1=0.0, scalar2=2.0, op0=ALU.is_ge, op1=ALU.mult)
+        nc.vector.tensor_scalar(out=t_fac[:, 0], in0=t_abs[:], scalar1=BIG, scalar2=1.0 / BIG, op0=ALU.min, op1=ALU.max)
+        nc.vector.tensor_scalar(out=t_fac[:, 1], in0=t_abs[:], scalar1=1.0 / BIG, scalar2=1.0, op0=ALU.mult, op1=ALU.max)
+        nc.vector.tensor_scalar(out=t_fac[:, 2], in0=t_abs[:], scalar1=BIG, scalar2=1.0, op0=ALU.mult, op1=ALU.min)
+        nc.vector.tensor_scalar(out=t_sgn[:], in0=t_pos[:], scalar1=-1.0, scalar2=None, op0=ALU.add)
+        nc.scalar.activation(out=t_log[:], in_=t_fac[:], func=ACT.Ln)
+        nc.scalar.activation(out=warm[:, 1:2], in_=ones[:], func=ACT.Tanh)
+
+        copy_q(0)
+        nc.vector.tensor_tensor(out=t_sum[:], in0=t_log[:, 0], in1=t_log[:, 1], op=ALU.add)
+        quant_q(0)
+        nc.vector.tensor_tensor(out=ln_t[:], in0=t_sum[:], in1=t_log[:, 2], op=ALU.add)
+        copy_k(0, 0)
+        copy_k(0, 1)
+        quant_k(0, 0)
+        quant_k(0, 1)
+        for u in range(3):
+            gate_tanh(u)
+        for g in range(G):
+            scores(0, g)
+        copy_q(1)
+        copy_v(0)
+        quant_q(1)
+
+        last = UNITS - 1
+        for p in range(-1, last):
+            u = p + 1
+            if p >= 0:
+                copy_w(p, 0, G)
+            if u == last:
+                cap(u, 0)
+                cap(u, 1)
+                weights(u, 0, 1)
+                cap(u, 2)
+                weights(u, 1, 2)
+                quant_w(p, 0, G)
+                values(p, 0, G)
+                cap(u, 3)
+                weights(u, 2, 3)
+                weights(u, 3, 4)
+                gate_tanh(u)
+                copy_w(u, 0, 1)
+                denom(p, 0, G)
+                quant_w(u, 0, 1)
+                values(u, 0, 1)
+                recip(p, 0, G)
+                gate_affine(p)
+                copy_w(u, 1, 2)
+                finish(p, 0, 0)
+                quant_w(u, 1, 2)
+                values(u, 1, 2)
+                finish(p, 0, 1)
+                copy_w(u, 2, 3)
+                finish(p, 0, 2)
+                quant_w(u, 2, 3)
+                values(u, 2, 3)
+                finish(p, 0, 3)
+                store(p, 0, G)
+                continue
+            for g in range(G - 1):
+                cap(u, g)
+                scores(u + 1, g)
+            if p + 3 <= last:
+                copy_q(p + 3)
+            if p >= 0:
+                quant_w(p, 0, G)
+                values(p, 0, G)
+            cap(u, G - 1)
+            scores(u + 1, G - 1)
+            if u + 3 < last:
+                gate_tanh(u + 3)
+                weights(u, 0, G)
+            else:
+                weights(u, 0, 2)
+                weights(u, 2, G)
+            if p < 0:
+                quant_v(0)
+                nc.vector.transpose(out=sink_q[:], in_=sink_raw[:])
+                quant_q(2)
+                continue
+            if p < 2:
+                copy_k(1, p)
+            if p == 2:
+                copy_v(1)
+            denom(p, 0, G)
+            gate_affine(p)
+            recip(p, 0, G)
+            if p + 3 <= last:
+                quant_q(p + 3)
+            if p < 2:
+                quant_k(1, p)
+            if p == 2:
+                quant_v(1)
+            for g in range(G):
+                finish(p, 0, g)
+            store(p, 0, G)
+
+        copy_w(last, 3, 4)
+        denom(last, 0, 3)
+        quant_w(last, 3, 4)
+        values(last, 3, 4)
+        recip(last, 0, 3)
+        gate_affine(last)
+        finish(last, 0, 0)
+        denom(last, 3, 4)
+        finish(last, 1, 1)
+        store(last, 0, 2)
+        recip(last, 3, 4)
+        finish(last, 2, 2)
+        finish(last, 3, 3)
+        store(last, 2, 4)

@@ -1,4 +1,5 @@
 from contextlib import ExitStack
+from itertools import product
 
 import concourse.mybir as mybir
 
@@ -23,6 +24,8 @@ CH = NQ // QT
 UNITS = KV * CH
 BIG = 2.0**62
 DEPTH = 3
+HEADS = ((2, 3, 4, 5), (0, 1, 6, 7))
+RUNS = (((0, 4),), ((0, 2), (2, 4)))
 
 
 def tile_rows_a_exp_cap_sink_gate_kernel(tc, qT, kT, t, v, sink, og, out):
@@ -45,21 +48,21 @@ def tile_rows_a_exp_cap_sink_gate_kernel(tc, qT, kT, t, v, sink, og, out):
         ones = mk("ones", [P, 1], F32)
         warm = mk("warm", [P, 2], F32)
         sink_raw = mk("sink_raw", [P, 32], F32)
-        sink_q = mk("sink_q", [P, 32], F32)
+        sink_q = mk("sink_q", [P, 48], F32)
 
-        k_raw = [mk("k_raw%d" % s, [P, PACK, NT], F32) for s in range(KV)]
-        k_bf = [mk("k_bf%d" % s, [P, PACK, P, PACK], BF16) for s in range(KV)]
-        k_codes = [mk("k_codes%d" % s, [P, NT], U32) for s in range(KV)]
-        k_scales = [mk("k_scales%d" % s, [P, NT], U8) for s in range(KV)]
+        k_raw = mk("k_raw", [P, PACK, NT], F32)
+        k_bf = mk("k_bf", [P, PACK, P, PACK], BF16)
+        k_codes = mk("k_codes", [P, NT], U32)
+        k_scales = mk("k_scales", [P, NT], U8)
         q_raw = [mk("q_raw%d" % s, [P, PACK, NQ], F32) for s in range(KV)]
         q_bf = [mk("q_bf%d" % u, [P, QT, PACK], BF16) for u in range(UNITS)]
         q_codes = [mk("q_codes%d" % u, [P, QT], U32) for u in range(UNITS)]
         q_scales = [mk("q_scales%d" % u, [P, QT], U8) for u in range(UNITS)]
-        v_raw = [mk("v_raw%d" % s, [P, PACK, D], F32) for s in range(KV)]
-        v_bf = [mk("v_bf%d" % s, [P, D, PACK], BF16) for s in range(KV)]
-        v_codes = [mk("v_codes%d" % s, [P, D], U32) for s in range(KV)]
-        v_scales = [mk("v_scales%d" % s, [P, D], U8) for s in range(KV)]
-        og_raw = [mk("og_raw%d" % s, [P, CH, G, D], F32) for s in range(KV)]
+        v_raw = mk("v_raw", [P, KV, PACK, D], F32)
+        v_bf = mk("v_bf", [P, KV, D, PACK], BF16)
+        v_codes = mk("v_codes", [P, KV * D], U32)
+        v_scales = mk("v_scales", [P, KV * D], U8)
+        og_raw = [mk("og_raw%d" % s, [P, G, CH, D], F32) for s in range(KV)]
         g_tanh = [mk("g_tanh%d" % u, [P, G, D], F32) for u in range(UNITS)]
         gate = [mk("gate%d" % u, [P, G, D], F32) for u in range(UNITS)]
         res = [mk("res%d" % u, [P, G, D], F32) for u in range(UNITS)]
@@ -74,63 +77,64 @@ def tile_rows_a_exp_cap_sink_gate_kernel(tc, qT, kT, t, v, sink, og, out):
         score = [ps.tile([P, PACK, QT], F32, name="score%d" % g) for g in range(G)]
         ybank = [ps.tile([P, G, D], F32, name="ybank%d" % i) for i in range(4)]
 
-        q_view = qT.rearrange("(s g) (p j) n -> s (g p) j n", g=G, j=PACK)
-        k_view = kT.rearrange("s (p j) n -> s p j n", j=PACK)
-        v_view = v.rearrange("s (p j) e -> s p j e", j=PACK)
-        og_view = og.rearrange("(s g) (c p) e -> s c p g e", g=G, p=P)
-        out_view = out.rearrange("(s g) (c p) e -> s c p g e", g=G, p=P)
+        q_view = qT.rearrange("h (p j) n -> (h p) j n", j=PACK)
+        k_view = kT.rearrange("s (p j) n -> (s p) j n", j=PACK)
+        og_view = og.rearrange("h (c p) e -> p h c e", p=P)
+        out_view = out.rearrange("h (c p) e -> p h c e", p=P)
 
         def load_q(s, c0, c1):
-            nc.sync.dma_start(out=q_raw[s][:, :, c0 * QT : c1 * QT], in_=q_view[s][:, :, c0 * QT : c1 * QT])
+            cols = slice(c0 * QT, c1 * QT)
+            for g0, g1 in RUNS[s]:
+                h0 = HEADS[s][g0]
+                src = q_view[ROWS * h0 : ROWS * (h0 + g1 - g0), :, cols]
+                nc.sync.dma_start(out=q_raw[s][ROWS * g0 : ROWS * g1, :, cols], in_=src)
 
-        def load_k(eng, s, g):
-            eng.dma_start(out=k_raw[s][ROWS * g : ROWS * (g + 1)], in_=k_view[s])
-
-        def load_og(u):
-            nc.sync.dma_start(out=og_raw[u // CH][:, u % CH], in_=og_view[u // CH][u % CH])
-
-        def load_v(s):
-            nc.sync.dma_start(out=v_raw[s][:], in_=v_view[s])
+        def load_og(s, c0, c1):
+            for g0, g1 in RUNS[s]:
+                h0 = HEADS[s][g0]
+                nc.sync.dma_start(out=og_raw[s][:, g0:g1, c0:c1], in_=og_view[:, h0 : h0 + g1 - g0, c0:c1])
 
         def quant(codes, scales, src):
             nc.vector.quantize_mx(out=codes.bitcast(FP8X4), scales=scales, in_=src)
 
         def copy_q(u):
             src = q_raw[u // CH][:, :, (u % CH) * QT : (u % CH + 1) * QT]
-            nc.vector.tensor_copy(out=q_bf[u][:], in_=src.rearrange("p j n -> p n j"))
+            nc.vector.tensor_copy(
+                out=q_bf[u][:].rearrange("p (m i) j -> p m j i", i=4), in_=src.rearrange("p j (m i) -> p m j i", i=4)
+            )
 
         def quant_q(u):
             quant(q_codes[u][:], q_scales[u][:], q_bf[u][:].rearrange("p n j -> p (n j)"))
 
-        def copy_k(s, half):
-            src = k_raw[s][:].rearrange("p j (m r) -> p r m j", r=PACK)
-            nc.vector.tensor_copy(out=k_bf[s][:, 2 * half : 2 * half + 2], in_=src[:, 2 * half : 2 * half + 2])
+        def copy_k():
+            nc.vector.tensor_copy(
+                out=k_bf[:].rearrange("p r m j -> p m j r"), in_=k_raw[:].rearrange("p j (m r) -> p m j r", r=PACK)
+            )
 
-        def quant_k(s, half):
+        def quant_k(half):
             cols = slice(2 * half * P, (2 * half + 2) * P)
-            src = k_bf[s][:, 2 * half : 2 * half + 2].rearrange("p r m j -> p (r m j)")
-            quant(k_codes[s][:, cols], k_scales[s][:, cols], src)
+            src = k_bf[:, 2 * half : 2 * half + 2].rearrange("p r m j -> p (r m j)")
+            quant(k_codes[:, cols], k_scales[:, cols], src)
 
         def copy_v(s):
             nc.vector.tensor_tensor(
-                out=v_bf[s][:],
-                in0=v_raw[s][:].rearrange("p r e -> p e r"),
+                out=v_bf[:, s],
+                in0=v_raw[:, s].rearrange("p r e -> p e r"),
                 in1=t_sgn[:].unsqueeze(1).to_broadcast([P, D, PACK]),
                 op=ALU.mult,
             )
 
-        def quant_v(s):
-            quant(v_codes[s][:], v_scales[s][:], v_bf[s][:].rearrange("p e r -> p (e r)"))
+        def quant_v():
+            quant(v_codes[:], v_scales[:], v_bf[:].rearrange("p s e r -> p (s e r)"))
 
-        def scores(u, g):
-            s = u // CH
-            rows = slice(ROWS * g, ROWS * (g + 1))
-            for r in range(PACK):
+        def scores(u, g0, g1):
+            for r, g in product(range(PACK), range(g0, g1)):
+                rows = slice(ROWS * g, ROWS * (g + 1))
                 cols = slice(r * P, (r + 1) * P)
                 nc.tensor.matmul_mx(
                     out=score[g][:, r, :],
-                    lhsT=k_codes[s][rows, cols].bitcast(FP8X4),
-                    lhsT_scale=k_scales[s][rows, cols],
+                    lhsT=k_codes[rows, cols].bitcast(FP8X4),
+                    lhsT_scale=k_scales[rows, cols],
                     rhs=q_codes[u][rows, :].bitcast(FP8X4),
                     rhs_scale=q_scales[u][rows, :],
                     start=True,
@@ -156,7 +160,7 @@ def tile_rows_a_exp_cap_sink_gate_kernel(tc, qT, kT, t, v, sink, og, out):
                 )
 
         def gate_tanh(u):
-            nc.scalar.activation(out=g_tanh[u][:], in_=og_raw[u // CH][:, u % CH], func=ACT.Tanh, scale=0.5)
+            nc.scalar.activation(out=g_tanh[u][:], in_=og_raw[u // CH][:, :, u % CH], func=ACT.Tanh, scale=0.5)
 
         def gate_affine(u):
             nc.vector.tensor_scalar(
@@ -166,7 +170,8 @@ def tile_rows_a_exp_cap_sink_gate_kernel(tc, qT, kT, t, v, sink, og, out):
         def copy_w(u, g0, g1):
             cols = slice(g0 * QT, g1 * QT)
             nc.vector.tensor_copy(
-                out=w_bf[u % 2][:, cols, :], in_=w_rows[u % DEPTH][:, :, cols].rearrange("p r n -> p n r")
+                out=w_bf[u % 2][:, cols, :].rearrange("p (m i) r -> p m r i", i=4),
+                in_=w_rows[u % DEPTH][:, :, cols].rearrange("p r (m i) -> p m r i", i=4),
             )
 
         def quant_w(u, g0, g1):
@@ -178,25 +183,31 @@ def tile_rows_a_exp_cap_sink_gate_kernel(tc, qT, kT, t, v, sink, og, out):
             return ybank[0 if (u, g0) == (UNITS - 1, G - 1) else u % 4]
 
         def values(u, g0, g1):
-            s = u // CH
             for g in range(g0, g1):
                 cols = slice(g * QT, (g + 1) * QT)
+                kv = slice(g // 2 * D, (g // 2 + 1) * D)
                 nc.tensor.matmul_mx(
                     out=bank(u, g0)[:, g, :],
                     lhsT=w_codes[u % 2][:, cols].bitcast(FP8X4),
                     lhsT_scale=w_scales[u % 2][:, cols],
-                    rhs=v_codes[s][:].bitcast(FP8X4),
-                    rhs_scale=v_scales[s][:],
+                    rhs=v_codes[:, kv].bitcast(FP8X4),
+                    rhs_scale=v_scales[:, kv],
                     start=True,
                     stop=True,
                 )
 
         def denom(u, g0, g1):
             s, c = divmod(u, CH)
-            sk = sink_q[:].rearrange("p (s g c) -> p s c g", s=KV, g=G)
-            nc.vector.tensor_tensor(
-                out=den[u][:, g0:g1], in0=bank(u, g0)[:, g0:g1, D - 1], in1=sk[:, s, c, g0:g1], op=ALU.add
-            )
+            y_last = bank(u, g0)[:, g0:g1, D - 1]
+            dst = den[u][:, g0:g1]
+            if s == 0 or g1 - g0 < G:
+                h0 = HEADS[s][g0]
+                sk = sink_q[:].rearrange("p (h c) -> p h c", c=CH)[:, h0 : h0 + g1 - g0, c]
+            else:
+                sk = sink_q[:].rearrange("p (a h c) -> p a h c", a=2, c=CH)[:, :, 0:2, c]
+                y_last = y_last.rearrange("p (a h) -> p a h", a=2)
+                dst = dst.rearrange("p (a h) -> p a h", a=2)
+            nc.vector.tensor_tensor(out=dst, in0=y_last, in1=sk, op=ALU.add)
 
         def recip(u, g0, g1):
             nc.vector.reciprocal(out=rec[u][:, g0:g1], in_=den[u][:, g0:g1])
@@ -212,31 +223,36 @@ def tile_rows_a_exp_cap_sink_gate_kernel(tc, qT, kT, t, v, sink, og, out):
             )
 
         def store(u, g0, g1):
-            nc.sync.dma_start(out=out_view[u // CH][u % CH][:, g0:g1, :], in_=res[u][:, g0:g1, :])
+            s, c = divmod(u, CH)
+            h0 = HEADS[s][g0]
+            nc.sync.dma_start(out=out_view[:, h0 : h0 + g1 - g0, c], in_=res[u][:, g0:g1, :])
+
+        def store_all(u):
+            for g0, g1 in RUNS[u // CH]:
+                store(u, g0, g1)
+
+        def epilogue(u):
+            denom(u, 0, G)
+            gate_affine(u)
+            recip(u, 0, G)
 
         ctx.enter_context(tc.manual_schedule())
 
         nc.scalar.dma_start(out=t_raw[:], in_=t.rearrange("(p r) o -> p (r o)", r=PACK))
+        nc.sync.dma_start(out=k_raw[0:ROWS], in_=k_view[0:ROWS])
+        nc.scalar.dma_start(out=k_raw[3 * ROWS : P], in_=k_view[ROWS : 2 * ROWS])
         load_q(0, 0, 1)
-        load_k(nc.scalar, 0, 2)
-        load_k(nc.sync, 0, 0)
-        load_k(nc.scalar, 0, 3)
-        load_k(nc.sync, 0, 1)
-        for u in range(3):
-            load_og(u)
+        nc.sync.dma_start(out=k_raw[ROWS : 3 * ROWS], in_=k_view)
+        for c in range(3):
+            load_og(0, c, c + 1)
         load_q(0, 1, 2)
-        load_v(0)
-        load_og(3)
+        nc.sync.dma_start(out=v_raw[:], in_=v.rearrange("s (p j) e -> p s j e", j=PACK))
         load_q(0, 2, 4)
         nc.sync.dma_start(out=sink_raw[:], in_=sink.rearrange("h (c a j) o -> a (h c) (j o)", c=CH, a=4))
-        for g in (0, 2, 1, 3):
-            load_k(nc.sync, 1, g)
-        load_og(4)
-        load_q(1, 0, 4)
-        load_og(5)
-        load_og(6)
-        load_v(1)
-        load_og(7)
+        load_q(1, 0, 2)
+        load_og(0, 3, 4)
+        load_og(1, 0, 4)
+        load_q(1, 2, 4)
 
         nc.gpsimd.memset(ones[:], 1.0)
         nc.scalar.activation(out=warm[:, 0:1], in_=ones[:], func=ACT.Ln)
@@ -253,93 +269,96 @@ def tile_rows_a_exp_cap_sink_gate_kernel(tc, qT, kT, t, v, sink, og, out):
         nc.vector.tensor_tensor(out=t_sum[:], in0=t_log[:, 0], in1=t_log[:, 1], op=ALU.add)
         quant_q(0)
         nc.vector.tensor_tensor(out=ln_t[:], in0=t_sum[:], in1=t_log[:, 2], op=ALU.add)
-        copy_k(0, 0)
-        copy_k(0, 1)
-        quant_k(0, 0)
-        quant_k(0, 1)
+        copy_k()
+        quant_k(0)
+        quant_k(1)
         for u in range(3):
             gate_tanh(u)
-        for g in range(G):
-            scores(0, g)
+        scores(0, 0, G)
         copy_q(1)
         copy_v(0)
         quant_q(1)
 
         last = UNITS - 1
-        for p in range(-1, last):
+        for p in range(-1, last - 1):
             u = p + 1
-            if p >= 0:
-                copy_w(p, 0, G)
-            if u == last:
-                cap(u, 0)
-                cap(u, 1)
-                weights(u, 0, 1)
-                cap(u, 2)
-                weights(u, 1, 2)
-                quant_w(p, 0, G)
-                values(p, 0, G)
-                cap(u, 3)
-                weights(u, 2, 3)
-                weights(u, 3, 4)
-                gate_tanh(u)
-                copy_w(u, 0, 1)
-                denom(p, 0, G)
-                quant_w(u, 0, 1)
-                values(u, 0, 1)
-                recip(p, 0, G)
-                gate_affine(p)
-                copy_w(u, 1, 2)
-                finish(p, 0, 0)
-                quant_w(u, 1, 2)
-                values(u, 1, 2)
-                finish(p, 0, 1)
-                copy_w(u, 2, 3)
-                finish(p, 0, 2)
-                quant_w(u, 2, 3)
-                values(u, 2, 3)
-                finish(p, 0, 3)
-                store(p, 0, G)
-                continue
-            for g in range(G - 1):
+            for g in range(G):
                 cap(u, g)
-                scores(u + 1, g)
-            if p + 3 <= last:
-                copy_q(p + 3)
-            if p >= 0:
-                quant_w(p, 0, G)
-                values(p, 0, G)
-            cap(u, G - 1)
-            scores(u + 1, G - 1)
-            if u + 3 < last:
-                gate_tanh(u + 3)
+                if g % 2 == 1:
+                    scores(u + 1, g - 1, g + 1)
+            if 2 <= u < last - 1:
+                gate_tanh(u + 1)
                 weights(u, 0, G)
             else:
                 weights(u, 0, 2)
                 weights(u, 2, G)
             if p < 0:
-                quant_v(0)
-                nc.vector.transpose(out=sink_q[:], in_=sink_raw[:])
+                copy_v(1)
+                copy_q(2)
+                quant_v()
+                nc.vector.transpose(out=sink_q[:, 0:32], in_=sink_raw[:])
                 quant_q(2)
                 continue
-            if p < 2:
-                copy_k(1, p)
-            if p == 2:
-                copy_v(1)
-            denom(p, 0, G)
-            gate_affine(p)
-            recip(p, 0, G)
-            if p + 3 <= last:
+            copy_w(p, 0, G)
+            if p > 0:
+                denom(p - 1, 0, G)
+                gate_affine(p - 1)
+                recip(p - 1, 0, G)
+            else:
+                copy_q(p + 3)
+            quant_w(p, 0, G)
+            values(p, 0, G)
+            if p > 0:
+                for g in range(G):
+                    finish(p - 1, 0, g)
+                store_all(p - 1)
+            if 0 < p <= last - 3:
+                copy_q(p + 3)
+            if p == last - 2:
+                gate_affine(p)
+                denom(p, 0, G)
+            if p <= last - 3:
                 quant_q(p + 3)
-            if p < 2:
-                quant_k(1, p)
-            if p == 2:
-                quant_v(1)
-            for g in range(G):
-                finish(p, 0, g)
-            store(p, 0, G)
+
+        p, u = last - 1, last
+        cap(u, 0)
+        cap(u, 1)
+        weights(u, 0, 1)
+        cap(u, 2)
+        weights(u, 1, 2)
+        cap(u, 3)
+        weights(u, 2, 3)
+        weights(u, 3, 4)
+        gate_tanh(u)
+        recip(p - 1, 0, G)
+        copy_w(p, 0, G)
+        finish(p - 1, 0, 0)
+        quant_w(p, 0, G)
+        values(p, 0, G)
+        for g in range(1, G):
+            finish(p - 1, 0, g)
+        store_all(p - 1)
+        copy_w(u, 0, 1)
+        denom(p, 0, G)
+        quant_w(u, 0, 1)
+        values(u, 0, 1)
+        recip(p, 0, G)
+        gate_affine(p)
+        copy_w(u, 1, 2)
+        finish(p, 0, 0)
+        quant_w(u, 1, 2)
+        values(u, 1, 2)
+        finish(p, 0, 1)
+        copy_w(u, 2, 3)
+        finish(p, 0, 2)
+        quant_w(u, 2, 3)
+        values(u, 2, 3)
+        finish(p, 0, 3)
+        store_all(p)
 
         copy_w(last, 3, 4)
-        denom(last, 0, 3)
+        denom(last, 0, 2)
+        denom(last, 2, 3)
         quant_w(last, 3, 4)
         values(last, 3, 4)
         recip(last, 0, 3)

@@ -106,9 +106,11 @@ def tile_rows_a_exp_cap_sink_gate_kernel(tc, qT, kT, t, v, sink, og, out):
         def quant_q(u):
             quant(q_codes[u][:], q_scales[u][:], q_bf[u][:].rearrange("p n j -> p (n j)"))
 
-        def copy_k():
+        def copy_k(half):
+            ms = slice(half * P // 2, (half + 1) * P // 2)
             nc.vector.tensor_copy(
-                out=k_bf[:].rearrange("p r m j -> p m j r"), in_=k_raw[:].rearrange("p j (m r) -> p m j r", r=PACK)
+                out=k_bf[:].rearrange("p r m j -> p m r j")[:, ms],
+                in_=k_raw[:].rearrange("p j (m r) -> p m r j", r=PACK)[:, ms],
             )
 
         def quant_k(half):
@@ -128,7 +130,7 @@ def tile_rows_a_exp_cap_sink_gate_kernel(tc, qT, kT, t, v, sink, og, out):
             quant(v_codes[:], v_scales[:], v_bf[:].rearrange("p s e r -> p (s e r)"))
 
         def scores(u, g0, g1):
-            for r, g in product(range(PACK), range(g0, g1)):
+            for r, g in product(range(PACK), reversed(range(g0, g1))):
                 rows = slice(ROWS * g, ROWS * (g + 1))
                 cols = slice(r * P, (r + 1) * P)
                 nc.tensor.matmul_mx(
@@ -222,10 +224,10 @@ def tile_rows_a_exp_cap_sink_gate_kernel(tc, qT, kT, t, v, sink, og, out):
                 op1=ALU.mult,
             )
 
-        def store(u, g0, g1):
+        def store(u, g0, g1, eng=nc.sync):
             s, c = divmod(u, CH)
             h0 = HEADS[s][g0]
-            nc.sync.dma_start(out=out_view[:, h0 : h0 + g1 - g0, c], in_=res[u][:, g0:g1, :])
+            eng.dma_start(out=out_view[:, h0 : h0 + g1 - g0, c], in_=res[u][:, g0:g1, :])
 
         def store_all(u):
             for g0, g1 in RUNS[u // CH]:
@@ -242,7 +244,9 @@ def tile_rows_a_exp_cap_sink_gate_kernel(tc, qT, kT, t, v, sink, og, out):
         nc.sync.dma_start(out=k_raw[0:ROWS], in_=k_view[0:ROWS])
         nc.scalar.dma_start(out=k_raw[3 * ROWS : P], in_=k_view[ROWS : 2 * ROWS])
         load_q(0, 0, 1)
-        nc.sync.dma_start(out=k_raw[ROWS : 3 * ROWS], in_=k_view)
+        for half in range(2):
+            toks = slice(half * NT // 2, (half + 1) * NT // 2)
+            nc.sync.dma_start(out=k_raw[ROWS : 3 * ROWS, :, toks], in_=k_view[:, :, toks])
         for c in range(3):
             load_og(0, c, c + 1)
         load_q(0, 1, 2)
@@ -269,7 +273,8 @@ def tile_rows_a_exp_cap_sink_gate_kernel(tc, qT, kT, t, v, sink, og, out):
         nc.vector.tensor_tensor(out=t_sum[:], in0=t_log[:, 0], in1=t_log[:, 1], op=ALU.add)
         quant_q(0)
         nc.vector.tensor_tensor(out=ln_t[:], in0=t_sum[:], in1=t_log[:, 2], op=ALU.add)
-        copy_k()
+        copy_k(0)
+        copy_k(1)
         quant_k(0)
         quant_k(1)
         for u in range(3):
@@ -308,12 +313,12 @@ def tile_rows_a_exp_cap_sink_gate_kernel(tc, qT, kT, t, v, sink, og, out):
                 copy_q(p + 3)
             quant_w(p, 0, G)
             values(p, 0, G)
+            if 0 < p <= last - 3:
+                copy_q(p + 3)
             if p > 0:
                 for g in range(G):
                     finish(p - 1, 0, g)
                 store_all(p - 1)
-            if 0 < p <= last - 3:
-                copy_q(p + 3)
             if p == last - 2:
                 gate_affine(p)
                 denom(p, 0, G)
@@ -369,5 +374,6 @@ def tile_rows_a_exp_cap_sink_gate_kernel(tc, qT, kT, t, v, sink, og, out):
         store(last, 0, 2)
         recip(last, 3, 4)
         finish(last, 2, 2)
+        store(last, 2, 3)
         finish(last, 3, 3)
-        store(last, 2, 4)
+        store(last, 3, 4, nc.scalar)

@@ -11,6 +11,7 @@ F32 = mybir.dt.float32
 BF16 = mybir.dt.bfloat16
 U32 = mybir.dt.uint32
 U8 = mybir.dt.uint8
+I32 = mybir.dt.int32
 FP8X4 = mybir.dt.float8_e4m3fn_x4
 ACT = mybir.ActivationFunctionType
 ALU = mybir.AluOpType
@@ -24,7 +25,9 @@ CH = NQ // QT
 UNITS = KV * CH
 BIG = 2.0**62
 DEPTH = 3
+CATCH = 4
 HEADS = ((2, 3, 4, 5), (0, 1, 6, 7))
+INNER, OUTER = (1, 2), (0, 3)
 RUNS = (((0, 4),), ((0, 2), (2, 4)))
 
 
@@ -129,8 +132,8 @@ def tile_rows_a_exp_cap_sink_gate_kernel(tc, qT, kT, t, v, sink, og, out):
         def quant_v():
             quant(v_codes[:], v_scales[:], v_bf[:].rearrange("p s e r -> p (s e r)"))
 
-        def scores(u, g0, g1):
-            for r, g in product(range(PACK), reversed(range(g0, g1))):
+        def scores(u, pair):
+            for r, g in product(range(PACK), reversed(pair)):
                 rows = slice(ROWS * g, ROWS * (g + 1))
                 cols = slice(r * P, (r + 1) * P)
                 nc.tensor.matmul_mx(
@@ -151,11 +154,11 @@ def tile_rows_a_exp_cap_sink_gate_kernel(tc, qT, kT, t, v, sink, og, out):
                 scale=1.0 / CAP,
             )
 
-        def weights(u, g0, g1):
-            for r in range(PACK):
+        def weights(u, tiles, slots=range(PACK)):
+            for r in slots:
                 nc.scalar.activation(
-                    out=w_rows[u % DEPTH][:, r, g0 * QT : g1 * QT].rearrange("p (g n) -> p g n", n=QT),
-                    in_=capped[u % 2][:, g0:g1, r, :],
+                    out=w_rows[u % DEPTH][:, r].rearrange("p (g n) -> p g n", n=QT)[:, tiles],
+                    in_=capped[u % 2][:, tiles, r, :],
                     func=ACT.Exp,
                     scale=CAP,
                     bias=ln_t[:, r : r + 1],
@@ -241,22 +244,15 @@ def tile_rows_a_exp_cap_sink_gate_kernel(tc, qT, kT, t, v, sink, og, out):
         ctx.enter_context(tc.manual_schedule())
 
         nc.scalar.dma_start(out=t_raw[:], in_=t.rearrange("(p r) o -> p (r o)", r=PACK))
-        nc.sync.dma_start(out=k_raw[0:ROWS], in_=k_view[0:ROWS])
-        nc.scalar.dma_start(out=k_raw[3 * ROWS : P], in_=k_view[ROWS : 2 * ROWS])
-        load_q(0, 0, 1)
         for half in range(2):
             toks = slice(half * NT // 2, (half + 1) * NT // 2)
             nc.sync.dma_start(out=k_raw[ROWS : 3 * ROWS, :, toks], in_=k_view[:, :, toks])
+        load_q(0, 0, 1)
         for c in range(3):
             load_og(0, c, c + 1)
         load_q(0, 1, 2)
-        nc.sync.dma_start(out=v_raw[:], in_=v.rearrange("s (p j) e -> p s j e", j=PACK))
-        load_q(0, 2, 4)
-        nc.sync.dma_start(out=sink_raw[:], in_=sink.rearrange("h (c a j) o -> a (h c) (j o)", c=CH, a=4))
-        load_q(1, 0, 2)
-        load_og(0, 3, 4)
-        load_og(1, 0, 4)
-        load_q(1, 2, 4)
+        nc.vector.memset(k_raw[0:ROWS].bitcast(I32), 0)
+        nc.vector.memset(k_raw[3 * ROWS : P].bitcast(I32), 0)
 
         nc.gpsimd.memset(ones[:], 1.0)
         nc.scalar.activation(out=warm[:, 0:1], in_=ones[:], func=ACT.Ln)
@@ -269,111 +265,145 @@ def tile_rows_a_exp_cap_sink_gate_kernel(tc, qT, kT, t, v, sink, og, out):
         nc.scalar.activation(out=t_log[:], in_=t_fac[:], func=ACT.Ln)
         nc.scalar.activation(out=warm[:, 1:2], in_=ones[:], func=ACT.Tanh)
 
-        copy_q(0)
-        nc.vector.tensor_tensor(out=t_sum[:], in0=t_log[:, 0], in1=t_log[:, 1], op=ALU.add)
-        quant_q(0)
-        nc.vector.tensor_tensor(out=ln_t[:], in0=t_sum[:], in1=t_log[:, 2], op=ALU.add)
         copy_k(0)
+        nc.vector.tensor_tensor(out=t_sum[:], in0=t_log[:, 0], in1=t_log[:, 1], op=ALU.add)
         copy_k(1)
+        copy_q(0)
         quant_k(0)
+        quant_q(0)
         quant_k(1)
-        for u in range(3):
-            gate_tanh(u)
-        scores(0, 0, G)
-        copy_q(1)
-        copy_v(0)
-        quant_q(1)
+        nc.vector.tensor_tensor(out=ln_t[:], in0=t_sum[:], in1=t_log[:, 2], op=ALU.add)
+        for dst, src in ((0, 1), (3, 2)):
+            nc.sync.dma_start(
+                out=k_codes[ROWS * dst : ROWS * (dst + 1)].bitcast(I32),
+                in_=k_codes[ROWS * src : ROWS * (src + 1)].bitcast(I32),
+            )
+            nc.sync.dma_start(
+                out=k_scales[ROWS * dst : ROWS * dst + 4].bitcast(I32),
+                in_=k_scales[ROWS * src : ROWS * src + 4].bitcast(I32),
+            )
+        nc.sync.dma_start(out=v_raw[:], in_=v.rearrange("s (p j) e -> p s j e", j=PACK))
+        load_q(0, 2, 4)
+        nc.sync.dma_start(out=sink_raw[:], in_=sink.rearrange("h (c a j) o -> a (h c) (j o)", c=CH, a=4))
+        load_q(1, 0, 2)
+        load_og(0, 3, 4)
+        load_og(1, 0, 4)
+        load_q(1, 2, 4)
 
+        inner, outer, every = slice(1, 3), slice(0, G, 3), slice(0, G)
         last = UNITS - 1
-        for p in range(-1, last - 1):
+
+        gate_tanh(0)
+        gate_tanh(1)
+        scores(0, INNER)
+        scores(0, OUTER)
+        copy_q(1)
+        gate_affine(0)
+        quant_q(1)
+        cap(0, 1)
+        cap(0, 2)
+        scores(1, INNER)
+        gate_tanh(2)
+        weights(0, inner, range(3))
+        cap(0, 0)
+        cap(0, 3)
+        scores(1, OUTER)
+        weights(0, inner, range(3, 4))
+        weights(0, outer)
+        copy_v(0)
+        copy_v(1)
+        copy_q(2)
+        quant_v()
+        nc.vector.transpose(out=sink_q[:, 0:32], in_=sink_raw[:])
+        quant_q(2)
+
+        for p in range(last - 1):
             u = p + 1
-            for g in range(G):
-                cap(u, g)
-                if g % 2 == 1:
-                    scores(u + 1, g - 1, g + 1)
+            late = p < CATCH
+            cap(u, 1)
+            cap(u, 2)
+            scores(u + 1, INNER)
+            cap(u, 0)
+            cap(u, 3)
+            if late:
+                scores(u + 1, OUTER)
             if 2 <= u < last - 1:
                 gate_tanh(u + 1)
-                weights(u, 0, G)
+                weights(u, every)
             else:
-                weights(u, 0, 2)
-                weights(u, 2, G)
-            if p < 0:
-                copy_v(1)
-                copy_q(2)
-                quant_v()
-                nc.vector.transpose(out=sink_q[:, 0:32], in_=sink_raw[:])
-                quant_q(2)
-                continue
+                weights(u, inner)
+                weights(u, outer)
             copy_w(p, 0, G)
-            if p > 0:
+            if 0 < p <= CATCH:
                 denom(p - 1, 0, G)
-                gate_affine(p - 1)
-                recip(p - 1, 0, G)
-            else:
+            if p + 3 <= last:
                 copy_q(p + 3)
+            else:
+                gate_affine(p + 1)
+            if 0 < p <= CATCH:
+                recip(p - 1, 0, G)
             quant_w(p, 0, G)
             values(p, 0, G)
-            if 0 < p <= last - 3:
-                copy_q(p + 3)
-            if p > 0:
+            if not late:
+                scores(u + 1, OUTER)
+            if p + 3 <= last:
+                quant_q(p + 3)
+            if 0 < p <= CATCH:
                 for g in range(G):
                     finish(p - 1, 0, g)
                 store_all(p - 1)
-            if p == last - 2:
-                gate_affine(p)
+            if not late:
                 denom(p, 0, G)
-            if p <= last - 3:
-                quant_q(p + 3)
+            if p + 3 <= last:
+                gate_affine(p + 1)
+            if not late:
+                recip(p, 0, G)
+                for g in range(G):
+                    finish(p, 0, g)
+                store_all(p)
 
         p, u = last - 1, last
-        cap(u, 0)
         cap(u, 1)
-        weights(u, 0, 1)
         cap(u, 2)
-        weights(u, 1, 2)
+        weights(u, slice(1, 2))
+        cap(u, 0)
+        weights(u, slice(2, 3))
         cap(u, 3)
-        weights(u, 2, 3)
-        weights(u, 3, 4)
+        weights(u, slice(0, 1))
+        weights(u, slice(3, 4))
         gate_tanh(u)
-        recip(p - 1, 0, G)
+        nc.scalar.activation(out=gate[u][:], in_=g_tanh[u][:], func=ACT.Copy, scale=0.5, bias=0.5)
         copy_w(p, 0, G)
-        finish(p - 1, 0, 0)
         quant_w(p, 0, G)
         values(p, 0, G)
-        for g in range(1, G):
-            finish(p - 1, 0, g)
-        store_all(p - 1)
-        copy_w(u, 0, 1)
-        denom(p, 0, G)
-        quant_w(u, 0, 1)
-        values(u, 0, 1)
-        recip(p, 0, G)
-        gate_affine(p)
         copy_w(u, 1, 2)
-        finish(p, 0, 0)
         quant_w(u, 1, 2)
         values(u, 1, 2)
-        finish(p, 0, 1)
         copy_w(u, 2, 3)
-        finish(p, 0, 2)
+        denom(p, 0, G)
         quant_w(u, 2, 3)
         values(u, 2, 3)
+        recip(p, 0, G)
+        finish(p, 0, 0)
+        finish(p, 0, 1)
+        copy_w(u, 0, 1)
+        finish(p, 0, 2)
+        quant_w(u, 0, 1)
+        values(u, 0, 1)
+        copy_w(u, 3, 4)
         finish(p, 0, 3)
         store_all(p)
-
-        copy_w(last, 3, 4)
-        denom(last, 0, 2)
-        denom(last, 2, 3)
-        quant_w(last, 3, 4)
-        values(last, 3, 4)
-        recip(last, 0, 3)
-        gate_affine(last)
-        finish(last, 0, 0)
-        denom(last, 3, 4)
-        finish(last, 1, 1)
-        store(last, 0, 2)
-        recip(last, 3, 4)
-        finish(last, 2, 2)
-        store(last, 2, 3)
-        finish(last, 3, 3)
-        store(last, 3, 4, nc.scalar)
+        quant_w(u, 3, 4)
+        values(u, 3, 4)
+        denom(u, 0, 2)
+        denom(u, 2, 3)
+        recip(u, 0, 3)
+        denom(u, 3, 4)
+        finish(u, 0, 0)
+        recip(u, 3, 4)
+        finish(u, 1, 1)
+        store(u, 0, 2)
+        finish(u, 2, 2)
+        store(u, 2, 3)
+        finish(u, 3, 3)
+        store(u, 3, 4, nc.scalar)

@@ -19,16 +19,26 @@ ALU = mybir.AluOpType
 P = 128
 PACK = 4
 ROWS = 32
-G = 4
+SCALE_ROWS = ROWS // 8
+TILES = P // ROWS
 QT = 128
-CH = NQ // QT
-UNITS = KV * CH
-BIG = 2.0**62
-DEPTH = 3
-CATCH = 4
+CHUNKS = NQ // QT
+SETS = H // TILES
+UNITS = SETS * CHUNKS
+LAST = UNITS - 1
+
 HEADS = ((2, 3, 4, 5), (0, 1, 6, 7))
-INNER, OUTER = (1, 2), (0, 3)
 RUNS = (((0, 4),), ((0, 2), (2, 4)))
+INNER, OUTER = (1, 2), (0, 3)
+INNER_TILES, OUTER_TILES, ALL_TILES = slice(1, 3), slice(0, TILES, 3), slice(0, TILES)
+
+LN_RANGE = 2.0**62
+ROW_BUFS = 3
+Y_BANKS = 4
+Q_AHEAD = 3
+CATCH_UP = LAST - Q_AHEAD
+RUN = 4
+SINK_STEP = (HEADS[1][2] - HEADS[1][0]) * CHUNKS
 
 
 def tile_rows_a_exp_cap_sink_gate_kernel(tc, qT, kT, t, v, sink, og, out):
@@ -37,104 +47,123 @@ def tile_rows_a_exp_cap_sink_gate_kernel(tc, qT, kT, t, v, sink, og, out):
         sb = ctx.enter_context(tc.tile_pool(name="sb", bufs=1))
         ps = ctx.enter_context(tc.psum_pool(name="ps", bufs=1))
 
-        def mk(name, shape, dtype):
+        def sbuf(name, shape, dtype):
             return sb.tile(shape, dtype, name=name, align_bytes=64)
 
-        t_raw = mk("t_raw", [P, PACK], F32)
-        t_abs = mk("t_abs", [P, PACK], F32)
-        t_fac = mk("t_fac", [P, 3, PACK], F32)
-        t_log = mk("t_log", [P, 3, PACK], F32)
-        t_sum = mk("t_sum", [P, PACK], F32)
-        ln_t = mk("ln_t", [P, PACK], F32)
-        t_pos = mk("t_pos", [P, PACK], F32)
-        t_sgn = mk("t_sgn", [P, PACK], F32)
-        ones = mk("ones", [P, 1], F32)
-        warm = mk("warm", [P, 2], F32)
-        sink_raw = mk("sink_raw", [P, 32], F32)
-        sink_q = mk("sink_q", [P, 48], F32)
+        def sbufs(name, count, shape, dtype):
+            return [sbuf("%s%d" % (name, i), shape, dtype) for i in range(count)]
 
-        k_raw = mk("k_raw", [P, PACK, NT], F32)
-        k_bf = mk("k_bf", [P, PACK, P, PACK], BF16)
-        k_codes = mk("k_codes", [P, NT], U32)
-        k_scales = mk("k_scales", [P, NT], U8)
-        q_raw = [mk("q_raw%d" % s, [P, PACK, NQ], F32) for s in range(KV)]
-        q_bf = [mk("q_bf%d" % u, [P, QT, PACK], BF16) for u in range(UNITS)]
-        q_codes = [mk("q_codes%d" % u, [P, QT], U32) for u in range(UNITS)]
-        q_scales = [mk("q_scales%d" % u, [P, QT], U8) for u in range(UNITS)]
-        v_raw = mk("v_raw", [P, KV, PACK, D], F32)
-        v_bf = mk("v_bf", [P, KV, D, PACK], BF16)
-        v_codes = mk("v_codes", [P, KV * D], U32)
-        v_scales = mk("v_scales", [P, KV * D], U8)
-        og_raw = [mk("og_raw%d" % s, [P, G, CH, D], F32) for s in range(KV)]
-        g_tanh = [mk("g_tanh%d" % u, [P, G, D], F32) for u in range(UNITS)]
-        gate = [mk("gate%d" % u, [P, G, D], F32) for u in range(UNITS)]
-        res = [mk("res%d" % u, [P, G, D], F32) for u in range(UNITS)]
-        den = [mk("den%d" % u, [P, G], F32) for u in range(UNITS)]
-        rec = [mk("rec%d" % u, [P, G], F32) for u in range(UNITS)]
-        capped = [mk("capped%d" % i, [P, G, PACK, QT], F32) for i in range(2)]
-        w_rows = [mk("w_rows%d" % i, [P, PACK, G * QT], BF16) for i in range(DEPTH)]
-        w_bf = [mk("w_bf%d" % i, [P, G * QT, PACK], BF16) for i in range(2)]
-        w_codes = [mk("w_codes%d" % i, [P, G * QT], U32) for i in range(2)]
-        w_scales = [mk("w_scales%d" % i, [P, G * QT], U8) for i in range(2)]
+        t_raw = sbuf("t_raw", [P, PACK], F32)
+        t_abs = sbuf("t_abs", [P, PACK], F32)
+        t_fac = sbuf("t_fac", [P, 3, PACK], F32)
+        t_log = sbuf("t_log", [P, 3, PACK], F32)
+        t_sum = sbuf("t_sum", [P, PACK], F32)
+        ln_t = sbuf("ln_t", [P, PACK], F32)
+        t_pos = sbuf("t_pos", [P, PACK], F32)
+        t_sgn = sbuf("t_sgn", [P, PACK], F32)
+        sink_raw = sbuf("sink_raw", [P, H * CHUNKS], F32)
+        sink_q = sbuf("sink_q", [P, 2 * SINK_STEP], F32)
 
-        score = [ps.tile([P, PACK, QT], F32, name="score%d" % g) for g in range(G)]
-        ybank = [ps.tile([P, G, D], F32, name="ybank%d" % i) for i in range(4)]
+        k_raw = sbuf("k_raw", [P, PACK, NT], F32)
+        k_bf = sbuf("k_bf", [P, PACK, P, PACK], BF16)
+        k_codes = sbuf("k_codes", [P, NT], U32)
+        k_scales = sbuf("k_scales", [P, NT], U8)
+        q_raw = sbufs("q_raw", SETS, [P, PACK, NQ], F32)
+        q_bf = sbufs("q_bf", UNITS, [P, QT, PACK], BF16)
+        q_codes = sbufs("q_codes", UNITS, [P, QT], U32)
+        q_scales = sbufs("q_scales", UNITS, [P, QT], U8)
+        v_raw = sbuf("v_raw", [P, KV, PACK, D], F32)
+        v_bf = sbuf("v_bf", [P, KV, D, PACK], BF16)
+        v_codes = sbuf("v_codes", [P, KV * D], U32)
+        v_scales = sbuf("v_scales", [P, KV * D], U8)
+        og_raw = sbufs("og_raw", SETS, [P, TILES, CHUNKS, D], F32)
+        g_tanh = sbufs("g_tanh", UNITS, [P, TILES, D], F32)
+        gate = sbufs("gate", UNITS, [P, TILES, D], F32)
+        res = sbufs("res", UNITS, [P, TILES, D], F32)
+        den = sbufs("den", UNITS, [P, TILES], F32)
+        rec = sbufs("rec", UNITS, [P, TILES], F32)
+        capped = sbufs("capped", 2, [P, TILES, PACK, QT], F32)
+        w_rows = sbufs("w_rows", ROW_BUFS, [P, PACK, TILES * QT], BF16)
+        w_bf = sbufs("w_bf", 2, [P, TILES * QT, PACK], BF16)
+        w_codes = sbufs("w_codes", 2, [P, TILES * QT], U32)
+        w_scales = sbufs("w_scales", 2, [P, TILES * QT], U8)
+
+        score = [ps.tile([P, PACK, QT], F32, name="score%d" % g) for g in range(TILES)]
+        y_banks = [ps.tile([P, TILES, D], F32, name="y_bank%d" % i) for i in range(Y_BANKS)]
 
         q_view = qT.rearrange("h (p j) n -> (h p) j n", j=PACK)
         k_view = kT.rearrange("s (p j) n -> (s p) j n", j=PACK)
         og_view = og.rearrange("h (c p) e -> p h c e", p=P)
         out_view = out.rearrange("h (c p) e -> p h c e", p=P)
 
+        def tile_rows(g0, g1):
+            return slice(ROWS * g0, ROWS * g1)
+
+        def tile_cols(g0, g1):
+            return slice(QT * g0, QT * g1)
+
         def load_q(s, c0, c1):
             cols = slice(c0 * QT, c1 * QT)
             for g0, g1 in RUNS[s]:
                 h0 = HEADS[s][g0]
                 src = q_view[ROWS * h0 : ROWS * (h0 + g1 - g0), :, cols]
-                nc.sync.dma_start(out=q_raw[s][ROWS * g0 : ROWS * g1, :, cols], in_=src)
+                nc.sync.dma_start(out=q_raw[s][tile_rows(g0, g1), :, cols], in_=src)
 
         def load_og(s, c0, c1):
             for g0, g1 in RUNS[s]:
                 h0 = HEADS[s][g0]
                 nc.sync.dma_start(out=og_raw[s][:, g0:g1, c0:c1], in_=og_view[:, h0 : h0 + g1 - g0, c0:c1])
 
-        def quant(codes, scales, src):
+        def quantise(codes, scales, src):
             nc.vector.quantize_mx(out=codes.bitcast(FP8X4), scales=scales, in_=src)
 
         def copy_q(u):
-            src = q_raw[u // CH][:, :, (u % CH) * QT : (u % CH + 1) * QT]
+            s, c = divmod(u, CHUNKS)
             nc.vector.tensor_copy(
-                out=q_bf[u][:].rearrange("p (m i) j -> p m j i", i=4), in_=src.rearrange("p j (m i) -> p m j i", i=4)
+                out=q_bf[u][:].rearrange("p (n i) j -> p n j i", i=RUN),
+                in_=q_raw[s][:, :, c * QT : (c + 1) * QT].rearrange("p j (n i) -> p n j i", i=RUN),
             )
 
         def quant_q(u):
-            quant(q_codes[u][:], q_scales[u][:], q_bf[u][:].rearrange("p n j -> p (n j)"))
+            quantise(q_codes[u][:], q_scales[u][:], q_bf[u][:].rearrange("p n j -> p (n j)"))
+
+        key_rows = tile_rows(0, 3)
 
         def copy_k(half):
-            ms = slice(half * P // 2, (half + 1) * P // 2)
+            words = slice(half * P // 2, (half + 1) * P // 2)
             nc.vector.tensor_copy(
-                out=k_bf[:].rearrange("p r m j -> p m r j")[:, ms],
-                in_=k_raw[:].rearrange("p j (m r) -> p m r j", r=PACK)[:, ms],
+                out=k_bf[key_rows].rearrange("p r m j -> p m r j")[:, words],
+                in_=k_raw[key_rows].rearrange("p j (m r) -> p m r j", r=PACK)[:, words],
             )
 
-        def quant_k(half):
-            cols = slice(2 * half * P, (2 * half + 2) * P)
-            src = k_bf[:, 2 * half : 2 * half + 2].rearrange("p r m j -> p (r m j)")
-            quant(k_codes[:, cols], k_scales[:, cols], src)
+        def quant_k(r):
+            cols = slice(r * P, (r + 1) * P)
+            src = k_bf[key_rows, r].rearrange("p m j -> p (m j)")
+            quantise(k_codes[key_rows, cols], k_scales[key_rows, cols], src)
 
-        def copy_v(s):
+        def spread_k(dst, src):
+            nc.sync.dma_start(
+                out=k_codes[tile_rows(dst, dst + 1)].bitcast(I32), in_=k_codes[tile_rows(src, src + 1)].bitcast(I32)
+            )
+            nc.sync.dma_start(
+                out=k_scales[ROWS * dst : ROWS * dst + SCALE_ROWS].bitcast(I32),
+                in_=k_scales[ROWS * src : ROWS * src + SCALE_ROWS].bitcast(I32),
+            )
+
+        def copy_v(kv):
             nc.vector.tensor_tensor(
-                out=v_bf[:, s],
-                in0=v_raw[:, s].rearrange("p r e -> p e r"),
+                out=v_bf[:, kv],
+                in0=v_raw[:, kv].rearrange("p r e -> p e r"),
                 in1=t_sgn[:].unsqueeze(1).to_broadcast([P, D, PACK]),
                 op=ALU.mult,
             )
 
         def quant_v():
-            quant(v_codes[:], v_scales[:], v_bf[:].rearrange("p s e r -> p (s e r)"))
+            quantise(v_codes[:], v_scales[:], v_bf[:].rearrange("p s e r -> p (s e r)"))
 
         def scores(u, pair):
             for r, g in product(range(PACK), reversed(pair)):
-                rows = slice(ROWS * g, ROWS * (g + 1))
+                rows = tile_rows(g, g + 1)
                 cols = slice(r * P, (r + 1) * P)
                 nc.tensor.matmul_mx(
                     out=score[g][:, r, :],
@@ -146,18 +175,19 @@ def tile_rows_a_exp_cap_sink_gate_kernel(tc, qT, kT, t, v, sink, og, out):
                     stop=True,
                 )
 
-        def cap(u, g):
-            nc.scalar.activation(
-                out=capped[u % 2][:, g].rearrange("p r n -> p (r n)"),
-                in_=score[g][:].rearrange("p r n -> p (r n)"),
-                func=ACT.Tanh,
-                scale=1.0 / CAP,
-            )
-
-        def weights(u, tiles, slots=range(PACK)):
-            for r in slots:
+        def cap(u, tiles):
+            for g in tiles:
                 nc.scalar.activation(
-                    out=w_rows[u % DEPTH][:, r].rearrange("p (g n) -> p g n", n=QT)[:, tiles],
+                    out=capped[u % 2][:, g].rearrange("p r n -> p (r n)"),
+                    in_=score[g][:].rearrange("p r n -> p (r n)"),
+                    func=ACT.Tanh,
+                    scale=1.0 / CAP,
+                )
+
+        def weights(u, tiles):
+            for r in range(PACK):
+                nc.scalar.activation(
+                    out=w_rows[u % ROW_BUFS][:, r].rearrange("p (g n) -> p g n", n=QT)[:, tiles],
                     in_=capped[u % 2][:, tiles, r, :],
                     func=ACT.Exp,
                     scale=CAP,
@@ -165,7 +195,8 @@ def tile_rows_a_exp_cap_sink_gate_kernel(tc, qT, kT, t, v, sink, og, out):
                 )
 
         def gate_tanh(u):
-            nc.scalar.activation(out=g_tanh[u][:], in_=og_raw[u // CH][:, :, u % CH], func=ACT.Tanh, scale=0.5)
+            s, c = divmod(u, CHUNKS)
+            nc.scalar.activation(out=g_tanh[u][:], in_=og_raw[s][:, :, c], func=ACT.Tanh, scale=0.5)
 
         def gate_affine(u):
             nc.vector.tensor_scalar(
@@ -173,237 +204,233 @@ def tile_rows_a_exp_cap_sink_gate_kernel(tc, qT, kT, t, v, sink, og, out):
             )
 
         def copy_w(u, g0, g1):
-            cols = slice(g0 * QT, g1 * QT)
+            cols = tile_cols(g0, g1)
             nc.vector.tensor_copy(
-                out=w_bf[u % 2][:, cols, :].rearrange("p (m i) r -> p m r i", i=4),
-                in_=w_rows[u % DEPTH][:, :, cols].rearrange("p r (m i) -> p m r i", i=4),
+                out=w_bf[u % 2][:, cols, :].rearrange("p (n i) r -> p n r i", i=RUN),
+                in_=w_rows[u % ROW_BUFS][:, :, cols].rearrange("p r (n i) -> p n r i", i=RUN),
             )
 
-        def quant_w(u, g0, g1):
-            cols = slice(g0 * QT, g1 * QT)
-            src = w_bf[u % 2][:, cols, :].rearrange("p n r -> p (n r)")
-            quant(w_codes[u % 2][:, cols], w_scales[u % 2][:, cols], src)
-
-        def bank(u, g0):
-            return ybank[0 if (u, g0) == (UNITS - 1, G - 1) else u % 4]
+        def y_bank(u, g):
+            return y_banks[0 if (u, g) == (LAST, TILES - 1) else u % Y_BANKS]
 
         def values(u, g0, g1):
+            cols = tile_cols(g0, g1)
+            src = w_bf[u % 2][:, cols, :].rearrange("p n r -> p (n r)")
+            quantise(w_codes[u % 2][:, cols], w_scales[u % 2][:, cols], src)
             for g in range(g0, g1):
-                cols = slice(g * QT, (g + 1) * QT)
-                kv = slice(g // 2 * D, (g // 2 + 1) * D)
+                head = tile_cols(g, g + 1)
+                kv = HEADS[u // CHUNKS][g] // (H // KV)
+                v_cols = slice(kv * D, (kv + 1) * D)
                 nc.tensor.matmul_mx(
-                    out=bank(u, g0)[:, g, :],
-                    lhsT=w_codes[u % 2][:, cols].bitcast(FP8X4),
-                    lhsT_scale=w_scales[u % 2][:, cols],
-                    rhs=v_codes[:, kv].bitcast(FP8X4),
-                    rhs_scale=v_scales[:, kv],
+                    out=y_bank(u, g0)[:, g, :],
+                    lhsT=w_codes[u % 2][:, head].bitcast(FP8X4),
+                    lhsT_scale=w_scales[u % 2][:, head],
+                    rhs=v_codes[:, v_cols].bitcast(FP8X4),
+                    rhs_scale=v_scales[:, v_cols],
                     start=True,
                     stop=True,
                 )
 
         def denom(u, g0, g1):
-            s, c = divmod(u, CH)
-            y_last = bank(u, g0)[:, g0:g1, D - 1]
+            s, c = divmod(u, CHUNKS)
+            sums = y_bank(u, g0)[:, g0:g1, D - 1]
             dst = den[u][:, g0:g1]
-            if s == 0 or g1 - g0 < G:
+            if s == 0 or g1 - g0 < TILES:
                 h0 = HEADS[s][g0]
-                sk = sink_q[:].rearrange("p (h c) -> p h c", c=CH)[:, h0 : h0 + g1 - g0, c]
+                sinks = sink_q[:].rearrange("p (h c) -> p h c", c=CHUNKS)[:, h0 : h0 + g1 - g0, c]
             else:
-                sk = sink_q[:].rearrange("p (a h c) -> p a h c", a=2, c=CH)[:, :, 0:2, c]
-                y_last = y_last.rearrange("p (a h) -> p a h", a=2)
+                sinks = sink_q[:].rearrange("p (a h c) -> p a h c", a=2, c=CHUNKS)[:, :, 0:2, c]
+                sums = sums.rearrange("p (a h) -> p a h", a=2)
                 dst = dst.rearrange("p (a h) -> p a h", a=2)
-            nc.vector.tensor_tensor(out=dst, in0=y_last, in1=sk, op=ALU.add)
+            nc.vector.tensor_tensor(out=dst, in0=sums, in1=sinks, op=ALU.add)
 
         def recip(u, g0, g1):
             nc.vector.reciprocal(out=rec[u][:, g0:g1], in_=den[u][:, g0:g1])
 
-        def finish(u, g0, g):
+        def finish(u, g):
             nc.vector.scalar_tensor_tensor(
                 out=res[u][:, g, :],
-                in0=bank(u, g0)[:, g, :],
+                in0=y_bank(u, g)[:, g, :],
                 scalar=rec[u][:, g : g + 1],
                 in1=gate[u][:, g, :],
                 op0=ALU.mult,
                 op1=ALU.mult,
             )
 
-        def store(u, g0, g1, eng=nc.sync):
-            s, c = divmod(u, CH)
+        def store(u, g0, g1, queue=nc.sync):
+            s, c = divmod(u, CHUNKS)
             h0 = HEADS[s][g0]
-            eng.dma_start(out=out_view[:, h0 : h0 + g1 - g0, c], in_=res[u][:, g0:g1, :])
+            queue.dma_start(out=out_view[:, h0 : h0 + g1 - g0, c], in_=res[u][:, g0:g1, :])
 
-        def store_all(u):
-            for g0, g1 in RUNS[u // CH]:
+        def store_unit(u):
+            for g0, g1 in RUNS[u // CHUNKS]:
                 store(u, g0, g1)
 
-        def epilogue(u):
-            denom(u, 0, G)
-            gate_affine(u)
-            recip(u, 0, G)
+        def finish_unit(u):
+            for g in range(TILES):
+                finish(u, g)
+            store_unit(u)
 
         ctx.enter_context(tc.manual_schedule())
 
         nc.scalar.dma_start(out=t_raw[:], in_=t.rearrange("(p r) o -> p (r o)", r=PACK))
         for half in range(2):
-            toks = slice(half * NT // 2, (half + 1) * NT // 2)
-            nc.sync.dma_start(out=k_raw[ROWS : 3 * ROWS, :, toks], in_=k_view[:, :, toks])
+            tokens = slice(half * NT // 2, (half + 1) * NT // 2)
+            nc.sync.dma_start(out=k_raw[tile_rows(1, 3), :, tokens], in_=k_view[:, :, tokens])
         load_q(0, 0, 1)
         for c in range(3):
             load_og(0, c, c + 1)
         load_q(0, 1, 2)
-        nc.vector.memset(k_raw[0:ROWS].bitcast(I32), 0)
-        nc.vector.memset(k_raw[3 * ROWS : P].bitcast(I32), 0)
+        nc.vector.memset(k_raw[tile_rows(0, 1)].bitcast(I32), 0)
+        nc.gpsimd.memset(k_scales[tile_rows(3, 4)].bitcast(I32), 0)
 
-        nc.gpsimd.memset(ones[:], 1.0)
-        nc.scalar.activation(out=warm[:, 0:1], in_=ones[:], func=ACT.Ln)
         nc.vector.scalar_tensor_tensor(out=t_abs[:], in0=t_raw[:], scalar=-1.0, in1=t_raw[:], op0=ALU.mult, op1=ALU.max)
         nc.vector.tensor_scalar(out=t_pos[:], in0=t_raw[:], scalar1=0.0, scalar2=2.0, op0=ALU.is_ge, op1=ALU.mult)
-        nc.vector.tensor_scalar(out=t_fac[:, 0], in0=t_abs[:], scalar1=BIG, scalar2=1.0 / BIG, op0=ALU.min, op1=ALU.max)
-        nc.vector.tensor_scalar(out=t_fac[:, 1], in0=t_abs[:], scalar1=1.0 / BIG, scalar2=1.0, op0=ALU.mult, op1=ALU.max)
-        nc.vector.tensor_scalar(out=t_fac[:, 2], in0=t_abs[:], scalar1=BIG, scalar2=1.0, op0=ALU.mult, op1=ALU.min)
+        factors = (
+            (LN_RANGE, 1.0 / LN_RANGE, ALU.min, ALU.max),
+            (1.0 / LN_RANGE, 1.0, ALU.mult, ALU.max),
+            (LN_RANGE, 1.0, ALU.mult, ALU.min),
+        )
+        for f, (first, second, op0, op1) in enumerate(factors):
+            nc.vector.tensor_scalar(out=t_fac[:, f], in0=t_abs[:], scalar1=first, scalar2=second, op0=op0, op1=op1)
         nc.vector.tensor_scalar(out=t_sgn[:], in0=t_pos[:], scalar1=-1.0, scalar2=None, op0=ALU.add)
         nc.scalar.activation(out=t_log[:], in_=t_fac[:], func=ACT.Ln)
-        nc.scalar.activation(out=warm[:, 1:2], in_=ones[:], func=ACT.Tanh)
 
         copy_k(0)
-        nc.vector.tensor_tensor(out=t_sum[:], in0=t_log[:, 0], in1=t_log[:, 1], op=ALU.add)
         copy_k(1)
         copy_q(0)
         quant_k(0)
         quant_q(0)
-        quant_k(1)
+        for r in range(1, PACK):
+            quant_k(r)
+        nc.vector.tensor_tensor(out=t_sum[:], in0=t_log[:, 0], in1=t_log[:, 1], op=ALU.add)
         nc.vector.tensor_tensor(out=ln_t[:], in0=t_sum[:], in1=t_log[:, 2], op=ALU.add)
-        for dst, src in ((0, 1), (3, 2)):
-            nc.sync.dma_start(
-                out=k_codes[ROWS * dst : ROWS * (dst + 1)].bitcast(I32),
-                in_=k_codes[ROWS * src : ROWS * (src + 1)].bitcast(I32),
-            )
-            nc.sync.dma_start(
-                out=k_scales[ROWS * dst : ROWS * dst + 4].bitcast(I32),
-                in_=k_scales[ROWS * src : ROWS * src + 4].bitcast(I32),
-            )
-        nc.sync.dma_start(out=v_raw[:], in_=v.rearrange("s (p j) e -> p s j e", j=PACK))
-        load_q(0, 2, 4)
-        nc.sync.dma_start(out=sink_raw[:], in_=sink.rearrange("h (c a j) o -> a (h c) (j o)", c=CH, a=4))
-        load_q(1, 0, 2)
-        load_og(0, 3, 4)
-        load_og(1, 0, 4)
-        load_q(1, 2, 4)
+        for dst, src in zip(OUTER, INNER):
+            spread_k(dst, src)
 
-        inner, outer, every = slice(1, 3), slice(0, G, 3), slice(0, G)
-        last = UNITS - 1
+        nc.sync.dma_start(out=v_raw[:], in_=v.rearrange("s (p r) e -> p s r e", r=PACK))
+        load_q(0, 2, CHUNKS)
+        nc.sync.dma_start(out=sink_raw[:], in_=sink.rearrange("h (c a y) o -> a (h c) (y o)", c=CHUNKS, a=TILES))
+        load_q(1, 0, 2)
+        load_og(0, 3, CHUNKS)
+        load_og(1, 0, CHUNKS)
+        load_q(1, 2, CHUNKS)
 
         gate_tanh(0)
         gate_tanh(1)
         scores(0, INNER)
-        scores(0, OUTER)
         copy_q(1)
         gate_affine(0)
         quant_q(1)
-        cap(0, 1)
-        cap(0, 2)
+        cap(0, INNER)
         scores(1, INNER)
+        scores(0, OUTER)
         gate_tanh(2)
-        weights(0, inner, range(3))
-        cap(0, 0)
-        cap(0, 3)
+        weights(0, INNER_TILES)
+        cap(1, INNER)
+        cap(0, OUTER)
         scores(1, OUTER)
-        weights(0, inner, range(3, 4))
-        weights(0, outer)
+        weights(1, INNER_TILES)
+        weights(0, OUTER_TILES)
+        cap(1, OUTER)
         copy_v(0)
         copy_v(1)
         copy_q(2)
         quant_v()
-        nc.vector.transpose(out=sink_q[:, 0:32], in_=sink_raw[:])
+        nc.vector.transpose(out=sink_q[:, 0 : H * CHUNKS], in_=sink_raw[:])
         quant_q(2)
+        copy_q(Q_AHEAD)
+        gate_affine(1)
+        quant_q(Q_AHEAD)
+        scores(2, INNER)
+        scores(2, OUTER)
+        cap(2, INNER)
+        weights(1, OUTER_TILES)
 
-        for p in range(last - 1):
+        for p in range(LAST - 1):
             u = p + 1
-            late = p < CATCH
-            cap(u, 1)
-            cap(u, 2)
-            scores(u + 1, INNER)
-            cap(u, 0)
-            cap(u, 3)
-            if late:
-                scores(u + 1, OUTER)
-            if 2 <= u < last - 1:
-                gate_tanh(u + 1)
-                weights(u, every)
-            else:
-                weights(u, inner)
-                weights(u, outer)
-            copy_w(p, 0, G)
-            if 0 < p <= CATCH:
-                denom(p - 1, 0, G)
-            if p + 3 <= last:
-                copy_q(p + 3)
-            else:
+            finish_previous = 0 < p <= CATCH_UP
+            finish_now = p >= CATCH_UP
+            more_queries = 0 < p <= LAST - Q_AHEAD
+            if u >= 2:
+                if u > 2:
+                    cap(u, INNER)
+                scores(u + 1, INNER)
+                cap(u, OUTER)
+                if not finish_now:
+                    scores(u + 1, OUTER)
+                if u + 1 < LAST:
+                    gate_tanh(u + 1)
+                    weights(u, ALL_TILES)
+                else:
+                    weights(u, INNER_TILES)
+                    weights(u, OUTER_TILES)
+            copy_w(p, 0, TILES)
+            if finish_previous:
+                denom(p - 1, 0, TILES)
+            if more_queries:
+                copy_q(p + Q_AHEAD)
+            elif p > 0:
                 gate_affine(p + 1)
-            if 0 < p <= CATCH:
-                recip(p - 1, 0, G)
-            quant_w(p, 0, G)
-            values(p, 0, G)
-            if not late:
+            if finish_previous:
+                recip(p - 1, 0, TILES)
+            values(p, 0, TILES)
+            if finish_now:
                 scores(u + 1, OUTER)
-            if p + 3 <= last:
-                quant_q(p + 3)
-            if 0 < p <= CATCH:
-                for g in range(G):
-                    finish(p - 1, 0, g)
-                store_all(p - 1)
-            if not late:
-                denom(p, 0, G)
-            if p + 3 <= last:
+            if more_queries:
+                quant_q(p + Q_AHEAD)
+            if finish_previous:
+                finish_unit(p - 1)
+            if finish_now:
+                denom(p, 0, TILES)
+            if more_queries:
                 gate_affine(p + 1)
-            if not late:
-                recip(p, 0, G)
-                for g in range(G):
-                    finish(p, 0, g)
-                store_all(p)
+            if finish_now:
+                recip(p, 0, TILES)
+                finish_unit(p)
 
-        p, u = last - 1, last
-        cap(u, 1)
-        cap(u, 2)
-        weights(u, slice(1, 2))
-        cap(u, 0)
-        weights(u, slice(2, 3))
-        cap(u, 3)
-        weights(u, slice(0, 1))
-        weights(u, slice(3, 4))
-        gate_tanh(u)
-        nc.scalar.activation(out=gate[u][:], in_=g_tanh[u][:], func=ACT.Copy, scale=0.5, bias=0.5)
-        copy_w(p, 0, G)
-        quant_w(p, 0, G)
-        values(p, 0, G)
-        copy_w(u, 1, 2)
-        quant_w(u, 1, 2)
-        values(u, 1, 2)
-        copy_w(u, 2, 3)
-        denom(p, 0, G)
-        quant_w(u, 2, 3)
-        values(u, 2, 3)
-        recip(p, 0, G)
-        finish(p, 0, 0)
-        finish(p, 0, 1)
-        copy_w(u, 0, 1)
-        finish(p, 0, 2)
-        quant_w(u, 0, 1)
-        values(u, 0, 1)
-        copy_w(u, 3, 4)
-        finish(p, 0, 3)
-        store_all(p)
-        quant_w(u, 3, 4)
-        values(u, 3, 4)
-        denom(u, 0, 2)
-        denom(u, 2, 3)
-        recip(u, 0, 3)
-        denom(u, 3, 4)
-        finish(u, 0, 0)
-        recip(u, 3, 4)
-        finish(u, 1, 1)
-        store(u, 0, 2)
-        finish(u, 2, 2)
-        store(u, 2, 3)
-        finish(u, 3, 3)
-        store(u, 3, 4, nc.scalar)
+        prev = LAST - 1
+        cap(LAST, INNER)
+        weights(LAST, slice(1, 2))
+        cap(LAST, (0,))
+        weights(LAST, slice(2, 3))
+        cap(LAST, (3,))
+        weights(LAST, slice(0, 1))
+        weights(LAST, slice(3, 4))
+        gate_tanh(LAST)
+        nc.scalar.activation(out=gate[LAST][:], in_=g_tanh[LAST][:], func=ACT.Copy, scale=0.5, bias=0.5)
+
+        copy_w(prev, 1, 3)
+        copy_w(prev, 0, 1)
+        values(prev, 1, 3)
+        copy_w(prev, 3, 4)
+        values(prev, 0, 1)
+        values(prev, 3, 4)
+        copy_w(LAST, 1, 2)
+        denom(prev, 0, TILES)
+        values(LAST, 1, 2)
+        recip(prev, 0, TILES)
+        copy_w(LAST, 2, 3)
+        finish(prev, 0)
+        values(LAST, 2, 3)
+        for g in range(1, TILES):
+            finish(prev, g)
+        store_unit(prev)
+        copy_w(LAST, 0, 1)
+        denom(LAST, 1, 2)
+        values(LAST, 0, 1)
+        copy_w(LAST, 3, 4)
+        denom(LAST, 2, 3)
+        values(LAST, 3, 4)
+        denom(LAST, 0, 1)
+        recip(LAST, 1, 3)
+        recip(LAST, 0, 1)
+        finish(LAST, 1)
+        finish(LAST, 2)
+        store(LAST, 2, 3)
+        denom(LAST, 3, 4)
+        finish(LAST, 0)
+        store(LAST, 0, 2)
+        recip(LAST, 3, 4)
+        finish(LAST, 3)
+        store(LAST, 3, 4, nc.scalar)

from contextlib import ExitStack
from itertools import product

import concourse.mybir as mybir

H, KV, D, NQ, NT = 8, 2, 128, 512, 512
CAP = 2.0
FLOPS = 2 * 2 * H * NQ * NT * D

F32 = mybir.dt.float32
BF16 = mybir.dt.bfloat16
U32 = mybir.dt.uint32
U8 = mybir.dt.uint8
I32 = mybir.dt.int32
FP8X4 = mybir.dt.float8_e4m3fn_x4
ACT = mybir.ActivationFunctionType
ALU = mybir.AluOpType

P = 128
PACK = 4
ROWS = 32
SCALE_ROWS = ROWS // 8
TILES = P // ROWS
QT = 128
CHUNKS = NQ // QT
SETS = H // TILES
UNITS = SETS * CHUNKS
LAST = UNITS - 1

HEADS = ((2, 3, 4, 5), (0, 1, 6, 7))
RUNS = (((0, 4),), ((0, 2), (2, 4)))
INNER, OUTER = (1, 2), (0, 3)
INNER_TILES, OUTER_TILES, ALL_TILES = slice(1, 3), slice(0, TILES, 3), slice(0, TILES)

LN_RANGE = 2.0**62
ROW_BUFS = 3
Y_BANKS = 4
Q_AHEAD = 3
CATCH_UP = LAST - Q_AHEAD
RUN = 4
SINK_STEP = (HEADS[1][2] - HEADS[1][0]) * CHUNKS


def tile_rows_a_exp_cap_sink_gate_kernel(tc, qT, kT, t, v, sink, og, out):
    nc = tc.nc
    with ExitStack() as ctx:
        sb = ctx.enter_context(tc.tile_pool(name="sb", bufs=1))
        ps = ctx.enter_context(tc.psum_pool(name="ps", bufs=1))

        def sbuf(name, shape, dtype):
            return sb.tile(shape, dtype, name=name, align_bytes=64)

        def sbufs(name, count, shape, dtype):
            return [sbuf("%s%d" % (name, i), shape, dtype) for i in range(count)]

        t_raw = sbuf("t_raw", [P, PACK], F32)
        t_abs = sbuf("t_abs", [P, PACK], F32)
        t_fac = sbuf("t_fac", [P, 3, PACK], F32)
        t_log = sbuf("t_log", [P, 3, PACK], F32)
        t_sum = sbuf("t_sum", [P, PACK], F32)
        ln_t = sbuf("ln_t", [P, PACK], F32)
        t_pos = sbuf("t_pos", [P, PACK], F32)
        t_sgn = sbuf("t_sgn", [P, PACK], F32)
        sink_raw = sbuf("sink_raw", [P, H * CHUNKS], F32)
        sink_q = sbuf("sink_q", [P, 2 * SINK_STEP], F32)

        k_raw = sbuf("k_raw", [P, PACK, NT], F32)
        k_bf = sbuf("k_bf", [P, PACK, P, PACK], BF16)
        k_codes = sbuf("k_codes", [P, NT], U32)
        k_scales = sbuf("k_scales", [P, NT], U8)
        q_raw = sbufs("q_raw", SETS, [P, PACK, NQ], F32)
        q_bf = sbufs("q_bf", UNITS, [P, QT, PACK], BF16)
        q_codes = sbufs("q_codes", UNITS, [P, QT], U32)
        q_scales = sbufs("q_scales", UNITS, [P, QT], U8)
        v_raw = sbuf("v_raw", [P, KV, PACK, D], F32)
        v_bf = sbuf("v_bf", [P, KV, D, PACK], BF16)
        v_codes = sbuf("v_codes", [P, KV * D], U32)
        v_scales = sbuf("v_scales", [P, KV * D], U8)
        og_raw = sbufs("og_raw", SETS, [P, TILES, CHUNKS, D], F32)
        g_tanh = sbufs("g_tanh", UNITS, [P, TILES, D], F32)
        gate = sbufs("gate", UNITS, [P, TILES, D], F32)
        res = sbufs("res", UNITS, [P, TILES, D], F32)
        den = sbufs("den", UNITS, [P, TILES], F32)
        rec = sbufs("rec", UNITS, [P, TILES], F32)
        capped = sbufs("capped", 2, [P, TILES, PACK, QT], F32)
        w_rows = sbufs("w_rows", ROW_BUFS, [P, PACK, TILES * QT], BF16)
        w_bf = sbufs("w_bf", 2, [P, TILES * QT, PACK], BF16)
        w_codes = sbufs("w_codes", 2, [P, TILES * QT], U32)
        w_scales = sbufs("w_scales", 2, [P, TILES * QT], U8)

        score = [ps.tile([P, PACK, QT], F32, name="score%d" % g) for g in range(TILES)]
        y_banks = [ps.tile([P, TILES, D], F32, name="y_bank%d" % i) for i in range(Y_BANKS)]

        q_view = qT.rearrange("h (p j) n -> (h p) j n", j=PACK)
        k_view = kT.rearrange("s (p j) n -> (s p) j n", j=PACK)
        og_view = og.rearrange("h (c p) e -> p h c e", p=P)
        out_view = out.rearrange("h (c p) e -> p h c e", p=P)

        def tile_rows(g0, g1):
            return slice(ROWS * g0, ROWS * g1)

        def tile_cols(g0, g1):
            return slice(QT * g0, QT * g1)

        def load_q(s, c0, c1):
            cols = slice(c0 * QT, c1 * QT)
            for g0, g1 in RUNS[s]:
                h0 = HEADS[s][g0]
                src = q_view[ROWS * h0 : ROWS * (h0 + g1 - g0), :, cols]
                nc.sync.dma_start(out=q_raw[s][tile_rows(g0, g1), :, cols], in_=src)

        def load_og(s, c0, c1):
            for g0, g1 in RUNS[s]:
                h0 = HEADS[s][g0]
                nc.sync.dma_start(out=og_raw[s][:, g0:g1, c0:c1], in_=og_view[:, h0 : h0 + g1 - g0, c0:c1])

        def quantise(codes, scales, src):
            nc.vector.quantize_mx(out=codes.bitcast(FP8X4), scales=scales, in_=src)

        def copy_q(u):
            s, c = divmod(u, CHUNKS)
            nc.vector.tensor_copy(
                out=q_bf[u][:].rearrange("p (n i) j -> p n j i", i=RUN),
                in_=q_raw[s][:, :, c * QT : (c + 1) * QT].rearrange("p j (n i) -> p n j i", i=RUN),
            )

        def quant_q(u):
            quantise(q_codes[u][:], q_scales[u][:], q_bf[u][:].rearrange("p n j -> p (n j)"))

        key_rows = tile_rows(0, 3)

        def copy_k(half):
            words = slice(half * P // 2, (half + 1) * P // 2)
            nc.vector.tensor_copy(
                out=k_bf[key_rows].rearrange("p r m j -> p m r j")[:, words],
                in_=k_raw[key_rows].rearrange("p j (m r) -> p m r j", r=PACK)[:, words],
            )

        def quant_k(r):
            cols = slice(r * P, (r + 1) * P)
            src = k_bf[key_rows, r].rearrange("p m j -> p (m j)")
            quantise(k_codes[key_rows, cols], k_scales[key_rows, cols], src)

        def spread_k(dst, src):
            nc.sync.dma_start(
                out=k_codes[tile_rows(dst, dst + 1)].bitcast(I32), in_=k_codes[tile_rows(src, src + 1)].bitcast(I32)
            )
            nc.sync.dma_start(
                out=k_scales[ROWS * dst : ROWS * dst + SCALE_ROWS].bitcast(I32),
                in_=k_scales[ROWS * src : ROWS * src + SCALE_ROWS].bitcast(I32),
            )

        def copy_v(kv):
            nc.vector.tensor_tensor(
                out=v_bf[:, kv],
                in0=v_raw[:, kv].rearrange("p r e -> p e r"),
                in1=t_sgn[:].unsqueeze(1).to_broadcast([P, D, PACK]),
                op=ALU.mult,
            )

        def quant_v():
            quantise(v_codes[:], v_scales[:], v_bf[:].rearrange("p s e r -> p (s e r)"))

        def scores(u, pair):
            for r, g in product(range(PACK), reversed(pair)):
                rows = tile_rows(g, g + 1)
                cols = slice(r * P, (r + 1) * P)
                nc.tensor.matmul_mx(
                    out=score[g][:, r, :],
                    lhsT=k_codes[rows, cols].bitcast(FP8X4),
                    lhsT_scale=k_scales[rows, cols],
                    rhs=q_codes[u][rows, :].bitcast(FP8X4),
                    rhs_scale=q_scales[u][rows, :],
                    start=True,
                    stop=True,
                )

        def cap(u, tiles):
            for g in tiles:
                nc.scalar.activation(
                    out=capped[u % 2][:, g].rearrange("p r n -> p (r n)"),
                    in_=score[g][:].rearrange("p r n -> p (r n)"),
                    func=ACT.Tanh,
                    scale=1.0 / CAP,
                )

        def weights(u, tiles):
            for r in range(PACK):
                nc.scalar.activation(
                    out=w_rows[u % ROW_BUFS][:, r].rearrange("p (g n) -> p g n", n=QT)[:, tiles],
                    in_=capped[u % 2][:, tiles, r, :],
                    func=ACT.Exp,
                    scale=CAP,
                    bias=ln_t[:, r : r + 1],
                )

        def gate_tanh(u):
            s, c = divmod(u, CHUNKS)
            nc.scalar.activation(out=g_tanh[u][:], in_=og_raw[s][:, :, c], func=ACT.Tanh, scale=0.5)

        def gate_affine(u):
            nc.vector.tensor_scalar(
                out=gate[u][:], in0=g_tanh[u][:], scalar1=0.5, scalar2=0.5, op0=ALU.mult, op1=ALU.add
            )

        def copy_w(u, g0, g1):
            cols = tile_cols(g0, g1)
            nc.vector.tensor_copy(
                out=w_bf[u % 2][:, cols, :].rearrange("p (n i) r -> p n r i", i=RUN),
                in_=w_rows[u % ROW_BUFS][:, :, cols].rearrange("p r (n i) -> p n r i", i=RUN),
            )

        def y_bank(u, g):
            return y_banks[0 if (u, g) == (LAST, TILES - 1) else u % Y_BANKS]

        def values(u, g0, g1):
            cols = tile_cols(g0, g1)
            src = w_bf[u % 2][:, cols, :].rearrange("p n r -> p (n r)")
            quantise(w_codes[u % 2][:, cols], w_scales[u % 2][:, cols], src)
            for g in range(g0, g1):
                head = tile_cols(g, g + 1)
                kv = HEADS[u // CHUNKS][g] // (H // KV)
                v_cols = slice(kv * D, (kv + 1) * D)
                nc.tensor.matmul_mx(
                    out=y_bank(u, g0)[:, g, :],
                    lhsT=w_codes[u % 2][:, head].bitcast(FP8X4),
                    lhsT_scale=w_scales[u % 2][:, head],
                    rhs=v_codes[:, v_cols].bitcast(FP8X4),
                    rhs_scale=v_scales[:, v_cols],
                    start=True,
                    stop=True,
                )

        def denom(u, g0, g1):
            s, c = divmod(u, CHUNKS)
            sums = y_bank(u, g0)[:, g0:g1, D - 1]
            dst = den[u][:, g0:g1]
            if s == 0 or g1 - g0 < TILES:
                h0 = HEADS[s][g0]
                sinks = sink_q[:].rearrange("p (h c) -> p h c", c=CHUNKS)[:, h0 : h0 + g1 - g0, c]
            else:
                sinks = sink_q[:].rearrange("p (a h c) -> p a h c", a=2, c=CHUNKS)[:, :, 0:2, c]
                sums = sums.rearrange("p (a h) -> p a h", a=2)
                dst = dst.rearrange("p (a h) -> p a h", a=2)
            nc.vector.tensor_tensor(out=dst, in0=sums, in1=sinks, op=ALU.add)

        def recip(u, g0, g1):
            nc.vector.reciprocal(out=rec[u][:, g0:g1], in_=den[u][:, g0:g1])

        def finish(u, g):
            nc.vector.scalar_tensor_tensor(
                out=res[u][:, g, :],
                in0=y_bank(u, g)[:, g, :],
                scalar=rec[u][:, g : g + 1],
                in1=gate[u][:, g, :],
                op0=ALU.mult,
                op1=ALU.mult,
            )

        def store(u, g0, g1, queue=nc.sync):
            s, c = divmod(u, CHUNKS)
            h0 = HEADS[s][g0]
            queue.dma_start(out=out_view[:, h0 : h0 + g1 - g0, c], in_=res[u][:, g0:g1, :])

        def store_unit(u):
            for g0, g1 in RUNS[u // CHUNKS]:
                store(u, g0, g1)

        def finish_unit(u):
            for g in range(TILES):
                finish(u, g)
            store_unit(u)

        ctx.enter_context(tc.manual_schedule())

        nc.scalar.dma_start(out=t_raw[:], in_=t.rearrange("(p r) o -> p (r o)", r=PACK))
        for half in range(2):
            tokens = slice(half * NT // 2, (half + 1) * NT // 2)
            nc.sync.dma_start(out=k_raw[tile_rows(1, 3), :, tokens], in_=k_view[:, :, tokens])
        load_q(0, 0, 1)
        for c in range(3):
            load_og(0, c, c + 1)
        load_q(0, 1, 2)
        nc.vector.memset(k_raw[tile_rows(0, 1)].bitcast(I32), 0)
        nc.gpsimd.memset(k_scales[tile_rows(3, 4)].bitcast(I32), 0)

        nc.vector.scalar_tensor_tensor(out=t_abs[:], in0=t_raw[:], scalar=-1.0, in1=t_raw[:], op0=ALU.mult, op1=ALU.max)
        nc.vector.tensor_scalar(out=t_pos[:], in0=t_raw[:], scalar1=0.0, scalar2=2.0, op0=ALU.is_ge, op1=ALU.mult)
        factors = (
            (LN_RANGE, 1.0 / LN_RANGE, ALU.min, ALU.max),
            (1.0 / LN_RANGE, 1.0, ALU.mult, ALU.max),
            (LN_RANGE, 1.0, ALU.mult, ALU.min),
        )
        for f, (first, second, op0, op1) in enumerate(factors):
            nc.vector.tensor_scalar(out=t_fac[:, f], in0=t_abs[:], scalar1=first, scalar2=second, op0=op0, op1=op1)
        nc.vector.tensor_scalar(out=t_sgn[:], in0=t_pos[:], scalar1=-1.0, scalar2=None, op0=ALU.add)
        nc.scalar.activation(out=t_log[:], in_=t_fac[:], func=ACT.Ln)

        copy_k(0)
        copy_k(1)
        copy_q(0)
        quant_k(0)
        quant_q(0)
        for r in range(1, PACK):
            quant_k(r)
        nc.vector.tensor_tensor(out=t_sum[:], in0=t_log[:, 0], in1=t_log[:, 1], op=ALU.add)
        nc.vector.tensor_tensor(out=ln_t[:], in0=t_sum[:], in1=t_log[:, 2], op=ALU.add)
        for dst, src in zip(OUTER, INNER):
            spread_k(dst, src)

        nc.sync.dma_start(out=v_raw[:], in_=v.rearrange("s (p r) e -> p s r e", r=PACK))
        load_q(0, 2, CHUNKS)
        nc.sync.dma_start(out=sink_raw[:], in_=sink.rearrange("h (c a y) o -> a (h c) (y o)", c=CHUNKS, a=TILES))
        load_q(1, 0, 2)
        load_og(0, 3, CHUNKS)
        load_og(1, 0, CHUNKS)
        load_q(1, 2, CHUNKS)

        gate_tanh(0)
        gate_tanh(1)
        scores(0, INNER)
        copy_q(1)
        gate_affine(0)
        quant_q(1)
        cap(0, INNER)
        scores(1, INNER)
        scores(0, OUTER)
        gate_tanh(2)
        weights(0, INNER_TILES)
        cap(1, INNER)
        cap(0, OUTER)
        scores(1, OUTER)
        weights(1, INNER_TILES)
        weights(0, OUTER_TILES)
        cap(1, OUTER)
        copy_v(0)
        copy_v(1)
        copy_q(2)
        quant_v()
        nc.vector.transpose(out=sink_q[:, 0 : H * CHUNKS], in_=sink_raw[:])
        quant_q(2)
        copy_q(Q_AHEAD)
        gate_affine(1)
        quant_q(Q_AHEAD)
        scores(2, INNER)
        scores(2, OUTER)
        cap(2, INNER)
        weights(1, OUTER_TILES)

        for p in range(LAST - 1):
            u = p + 1
            finish_previous = 0 < p <= CATCH_UP
            finish_now = p >= CATCH_UP
            more_queries = 0 < p <= LAST - Q_AHEAD
            if u >= 2:
                if u > 2:
                    cap(u, INNER)
                scores(u + 1, INNER)
                cap(u, OUTER)
                if not finish_now:
                    scores(u + 1, OUTER)
                if u + 1 < LAST:
                    gate_tanh(u + 1)
                    weights(u, ALL_TILES)
                else:
                    weights(u, INNER_TILES)
                    weights(u, OUTER_TILES)
            copy_w(p, 0, TILES)
            if finish_previous:
                denom(p - 1, 0, TILES)
            if more_queries:
                copy_q(p + Q_AHEAD)
            elif p > 0:
                gate_affine(p + 1)
            if finish_previous:
                recip(p - 1, 0, TILES)
            values(p, 0, TILES)
            if finish_now:
                scores(u + 1, OUTER)
            if more_queries:
                quant_q(p + Q_AHEAD)
            if finish_previous:
                finish_unit(p - 1)
            if finish_now:
                denom(p, 0, TILES)
            if more_queries:
                gate_affine(p + 1)
            if finish_now:
                recip(p, 0, TILES)
                finish_unit(p)

        prev = LAST - 1
        cap(LAST, INNER)
        weights(LAST, slice(1, 2))
        cap(LAST, (0,))
        weights(LAST, slice(2, 3))
        cap(LAST, (3,))
        weights(LAST, slice(0, 1))
        weights(LAST, slice(3, 4))
        gate_tanh(LAST)
        nc.scalar.activation(out=gate[LAST][:], in_=g_tanh[LAST][:], func=ACT.Copy, scale=0.5, bias=0.5)

        copy_w(prev, 1, 3)
        copy_w(prev, 0, 1)
        values(prev, 1, 3)
        copy_w(prev, 3, 4)
        values(prev, 0, 1)
        values(prev, 3, 4)
        copy_w(LAST, 1, 2)
        denom(prev, 0, TILES)
        values(LAST, 1, 2)
        recip(prev, 0, TILES)
        copy_w(LAST, 2, 3)
        finish(prev, 0)
        values(LAST, 2, 3)
        for g in range(1, TILES):
            finish(prev, g)
        store_unit(prev)
        copy_w(LAST, 0, 1)
        denom(LAST, 1, 2)
        values(LAST, 0, 1)
        copy_w(LAST, 3, 4)
        denom(LAST, 2, 3)
        values(LAST, 3, 4)
        denom(LAST, 0, 1)
        recip(LAST, 1, 3)
        recip(LAST, 0, 1)
        finish(LAST, 1)
        finish(LAST, 2)
        store(LAST, 2, 3)
        denom(LAST, 3, 4)
        finish(LAST, 0)
        store(LAST, 0, 2)
        recip(LAST, 3, 4)
        finish(LAST, 3)
        store(LAST, 3, 4, nc.scalar)
